import numpy as np, ml_dtypes
CORES = [10,34,74,98]
N = 4
BF = ml_dtypes.bfloat16
def gentries(a):
    return np.ascontiguousarray(a.reshape(8, 16, -1).transpose(0, 2, 1)).reshape(8, -1)
def gtable(e):
    e = np.asarray(e); return np.ascontiguousarray(e.reshape(8, -1, 16).transpose(0, 2, 1)).reshape(128, -1).astype(np.int32)
R0, P0, S, L, RO = 6144, 416, 32, 14, 3
P = P0 + RO * S; R = R0 + RO * (N - 1) * S
def counts(rng, share):
    return np.where(rng.random((N, 8, P0)) < share, rng.integers(L, 17, (N, 8, P0)), rng.integers(1, L, (N, 8, P0)))
def world(rng, cnt):
    post = rng.integers(0, R0, (N, 8, P0, 16)); home = np.full((N, 8, R0), 65535)
    on = np.argsort(rng.random((N, 8, P0, 16)), axis=-1) < cnt[..., None]
    for q in range(N):
        for g in range(8):
            ix = np.flatnonzero(on[q, g])[:R0]; c = rng.permutation(R0); n = len(ix)
            post[q, g].reshape(-1)[ix] = c[:n]; home[q, g, c[:n]] = ix
            if n: home[q, g, c[n:]] = np.where(rng.random(R0 - n) < 0.5, 65535, ix[rng.integers(0, n, R0 - n)])
    cl = rng.integers(0, 24, (N, 8, P0)); pr = rng.integers(40, 200, (8, 24, 14)); gi = np.arange(8)[None, :, None]
    at = np.minimum(home >> 4, P0 - 1)
    kc = np.where(home == 65535, rng.integers(0, 24, home.shape), np.take_along_axis(cl, at, 2))
    x = np.clip(pr[gi, kc] + rng.integers(-40, 41, (N, 8, R0, 14)), 0, 255)
    cen = rng.integers(0, 256, (N, 8, P0, 16)); cen[..., :14] = pr[gi, cl] + rng.integers(-16, 17, (N, 8, P0, 14))
    m = N * P0; w = m // 24; od = np.argsort(cl.transpose(1, 0, 2).reshape(8, m) + rng.random((8, m)), axis=1); pos = np.argsort(od, axis=1)
    z = np.take_along_axis(od, ((pos[:, :, None] + rng.integers(-w, w + 1, (8, m, 16))) % m).reshape(8, 16 * m), 1)
    near = (P * (z // P0) + z % P0).reshape(8, N, P0, 16).transpose(1, 0, 2, 3)
    near = np.where(rng.random(near.shape) < 0.15, rng.integers(0, N * P, near.shape), near)
    sl = 16 * at[:, :, None, :] + rng.integers(0, 16, (N, 8, RO, R0))
    ab = np.take_along_axis(post.reshape(N, 8, 16 * P0), sl.reshape(N, 8, RO * R0), 2).reshape(N, 8, RO, R0); u = rng.random(ab.shape)
    ab = np.where(u < 0.3, np.arange(R0), np.where(u < 0.5, rng.integers(0, R, ab.shape), ab))
    return {"x": x, "home": home, "cen": cen, "post": post, "near": near, "ab": ab}
def pack(d):
    h = d["home"][..., None]; v = np.concatenate([d["x"], h >> 8, h & 255], axis=-1).astype(np.float32)
    def turn(a): return np.ascontiguousarray(a.transpose(0, 1, 3, 2)).reshape(N, 128, -1)
    return {"rec": turn(v).astype(BF), "post": turn(d["post"]).astype(np.int32), "cen": turn(d["cen"].astype(np.float32)).astype(BF), "near": turn(d["near"]).astype(np.int32),
            "absorb": np.stack([gtable(a.reshape(8, -1)) for a in d["ab"]])}
def setup_inputs(rng):
    return pack(world(rng, counts(rng, rng.choice(np.array([0.2, 0.4, 0.6]), (N, 8, 1)))))
def setup_inputs_room(rng):
    nf = rng.choice(np.array([0, 1, S - 1, S, S + 1, 3 * S]), (N, 8)); nf[0] = (S, S + 1, S - 1, 0, 1, 3 * S, S, 2 * S); nf[1, 0] = S
    fm = np.argsort(rng.random((N, 8, P0)), axis=-1) < nf[..., None]
    cnt = np.where(fm, rng.choice(np.array([L, 16]), fm.shape), np.where(rng.random(fm.shape) < 0.5, L - 1, rng.integers(1, L, fm.shape)))
    d = world(rng, cnt); d["x"][:, 0] = rng.integers(128, 256, (N, R0, 14)); d["cen"][:, 0, :, :14] = 0
    fp = np.flatnonzero(fm[1, 0]); fq = np.flatnonzero(~fm[0, 0])
    d["near"][0, 0, fq] = (P + fp[np.arange(len(fq)) % S])[:, None]
    return pack(d)
def setup_inputs_ties(rng):
    cnt = counts(rng, 0.5); cnt[:, :, :6] = 16
    d = world(rng, cnt); d["x"] = rng.integers(0, 3, (N, 8, R0, 14)); d["cen"][..., :14] = rng.integers(0, 3, (N, 8, P0, 14))
    d["x"][:, 0] = 7; d["cen"][:, 0, :, :14] = np.where(rng.random((N, P0, 1)) < 0.5, 7, rng.integers(5, 9, (N, P0, 14)))
    d["x"][:, 2] *= rng.random((N, R0, 1)) < 0.5; d["cen"][:, 2, :, :14] = rng.integers(5, 9, (N, P0, 14))
    d["ab"][:, :4] = np.arange(R0)
    d["near"][:, 1::2] = P * rng.integers(0, N, (N, 4, P0, 16)) + rng.integers(0, 6, (N, 4, P0, 16))
    return pack(d)
def setup_inputs_ends(rng):
    q = rng.permutation(N); cnt = counts(rng, 0.3); cnt[q[0]] = rng.integers(0, L, (8, P0)); cnt[q[1]] = L
    ch = rng.permutation(P0)[:5]; cnt[:, 3] = rng.integers(1, L, (N, P0)); cnt[:, 3, ch] = 16
    cnt[:, 4] = rng.integers(1, L, (N, P0)); cnt[:, 4, 0] = 16; cnt[:, 4, P0 - 1] = L
    d = world(rng, cnt); ab = d["ab"]; near = d["near"]; d["cen"][:, 3, :, :14] = 0
    ab[:, 1] = rng.choice(np.array([0, R0 - 1]), (N, RO, R0)); ab[:, 2] = rng.integers(R0, R, (N, RO, R0)); ab[:, 5] = rng.integers(0, R0, (N, 1, 1)); ab[:, 3] = np.arange(R0)
    near[:, 4] = P * rng.integers(0, N, (N, P0, 16)) + rng.choice(np.array([0, P0 - 1, P0, P - 1]), (N, P0, 16))
    near[:, 3] = P * rng.integers(0, N, (N, P0, 16)) + np.where(rng.random((N, P0, 16)) < 0.5, P0 + rng.integers(0, 5, (N, P0, 16)), ch[rng.integers(0, 5, (N, P0, 16))])
    for a in range(N):
        s = d["post"][a, 3, ch]; d["x"][a, 3, s[:, 0]] = 0; d["x"][a, 3, s[:, 1:].reshape(-1)] = rng.integers(200, 256, (75, 14))
    return pack(d)
def setup_inputs_sharp(rng):
    d = world(rng, counts(rng, 0.4)); E = N * S - 32; n = P0 - S; i = np.arange(n)
    tg = np.where(i < n - 32, i % E, E + i - (n - 32))
    for g in range(0, 8, 2):
        fs = [np.sort(rng.permutation(P0)[:S]) for q in range(N)]; to = np.concatenate([P * q + fs[q] for q in range(N)])
        for q in range(N):
            fp = fs[q]; fq = np.setdiff1d(np.arange(P0), fp); po = d["post"][q, g]
            dull = (rng.random(n) < 0.5) & ((i < E) | ((i >= 2 * E) & (i < n - 32)))
            z = int(np.flatnonzero(tg == q * S)[0]); dull[z] = False
            cnt = np.zeros(P0, np.int64); cnt[fp] = rng.integers(L, 16, S); cnt[fq] = rng.integers(1, 5, n); cnt[fq[z]] = 1
            key = rng.random((P0, 16)); key[fp, 0] = 2
            on = np.argsort(np.argsort(key, axis=1), axis=1) < cnt[:, None]
            ix = np.flatnonzero(on); m = len(ix); c = 1 + rng.permutation(R0 - 1); dead = c[m:]; low = dead[:len(dead) // 2]; high = dead[len(dead) // 2:]
            po[fp] = rng.choice(high, (S, 16)); po[fq] = rng.choice(low, (n, 16))
            po[on] = c[:m]; po[fq[z], int(np.argmax(on[fq[z]]))] = 0
            h = np.where(rng.random(R0) < 0.5, 65535, ix[rng.integers(0, m, R0)]); h[po[on]] = ix; d["home"][q, g] = h
            x = rng.integers(130, 201, (R0, 14)); x[low] = 0; x[high] = 255
            e = fp[::2]; x[po[e][on[e]]] = 0
            e = fp[1::2]; s = po[e][on[e]]; x[s] = rng.integers(0, 3, (len(s), 14))
            e = fq[~dull]; x[po[e][on[e]]] = 127
            d["x"][q, g] = x; d["cen"][q, g, fq, :14] = 255; d["ab"][q, g, 0] = np.arange(R0)
            d["near"][q, g, fq] = np.where(np.arange(16) < rng.integers(0, 15, (n, 1)), (P * q + fq)[:, None], to[tg][:, None])
    return pack(d)
def setup_inputs_spread(rng):
    d = world(rng, counts(rng, rng.random((N, 8, 1))))
    d["x"] = np.minimum((np.exp2(8 * rng.random((N, 8, R0, 1))) * rng.random((N, 8, R0, 14))).astype(np.int64), 255)
    d["cen"] = rng.integers(0, 256, (N, 8, P0, 16)) >> rng.integers(0, 8, (N, 8, P0, 1))
    d["near"] = rng.integers(0, N * P, (N, 8, P0, 16)); d["ab"] = rng.integers(0, R, (N, 8, RO, R0))
    return pack(d)
def check_inputs(d):
    bad = []
    for k, hi in (("rec", 255), ("cen", 255), ("post", R0 - 1), ("near", N * P - 1), ("absorb", R - 1)):
        v = np.asarray(d[k]).astype(np.float64)
        if not (np.min(v) >= 0 and np.max(v) <= hi) or np.any(v != np.floor(v)): bad.append("range of " + k)
    v = np.asarray(d["rec"]).astype(np.float64).reshape(N, 8, 16, R0); h = v[:, :, 14] * 256 + v[:, :, 15]
    if np.any((h >= 16 * P0) & (h != 65535)): bad.append("homes of rec")
    return bad
def reference(rec, post, cen, near, absorb):
    w = rec.astype(np.float32).astype(np.int32).reshape(N, 8, 16, R0)
    x = np.zeros((N, 8, 14, R), np.int32); x[..., :R0] = w[:, :, :14]
    home = np.full((N, 8, R), 65535, np.int64); home[..., :R0] = w[:, :, 14] * 256 + w[:, :, 15]
    po = np.zeros((N, 8, P, 16), np.int64); po[:, :, :P0] = post.reshape(N, 8, 16, P0).transpose(0, 1, 3, 2)
    ne = np.zeros((N, 8, P, 16), np.int64); ne[:, :, :P0] = near.reshape(N, 8, 16, P0).transpose(0, 1, 3, 2)
    ce = np.zeros((N, 8, 14, P), np.int32); ce[..., :P0] = cen.astype(np.float32).astype(np.int32).reshape(N, 8, 16, P0)[:, :, :14]
    al = np.stack([gentries(a) for a in absorb]).astype(np.int64).reshape(N, 8, RO, R0)
    for t in range(RO):
        new = P0 + S * t
        for q in range(N): x[q, :, :, :R0] = np.maximum(x[q, :, :, :R0], np.take_along_axis(x[q], al[q, :, t][:, None, :], 2))
        live = (np.take_along_axis(home, po.reshape(N, 8, 16 * P), 2) == np.arange(16 * P)).reshape(N, 8, P, 16)
        full = (np.add.reduce(live.astype(np.int64), axis=3) >= L).astype(np.int64)
        num = np.add.accumulate(full, axis=2) - full; sp = (full == 1) & (num < S)
        b = np.zeros((N, 8, S, 14), np.int32); row = np.zeros((N, 8, S), np.int64)
        for q in range(N):
            for g in range(8):
                for k, p in enumerate(np.flatnonzero(sp[q, g])):
                    f = new + k; ix = po[q, g, p].copy(); v = x[q, g][:, ix]; on = live[q, g, p]
                    va = v[:, np.argmax(on)]; da = np.add.reduce(np.abs(v - va[:, None]), axis=0)
                    vb = v[:, np.argmax(np.where(on, da, -1))]; db = np.add.reduce(np.abs(v - vb[:, None]), axis=0)
                    go = on & (db < da)
                    po[q, g, f] = ix; ne[q, g, f] = ne[q, g, p]; ce[q, g, :, p] = va; ce[q, g, :, f] = vb
                    home[q, g, ix[go]] = 16 * f + np.flatnonzero(go)
                    b[q, g, k] = vb; row[q, g, k] = np.argmin(go)
        tab = np.where(sp, num + S * np.arange(N)[:, None, None], -1).transpose(1, 0, 2).reshape(8, N * P)
        mov = np.full((N, 8, N * S), -1, np.int64)
        for q in range(N):
            tj = np.take_along_axis(tab, ne[q].reshape(8, 16 * P), 1).reshape(8, P, 16)
            tg = np.take_along_axis(tj, np.argmax(tj >= 0, axis=2)[:, :, None], 2)[:, :, 0]
            for g in range(8):
                Q = np.flatnonzero((tg[g] >= 0) & ~sp[q, g]); v = x[q, g][:, po[q, g, Q]]
                vb = b[:, g].reshape(N * S, 14).T[:, tg[g, Q]]
                gain = np.add.reduce(np.abs(v - ce[q, g][:, Q][:, :, None]), axis=0) - np.add.reduce(np.abs(v - vb[:, :, None]), axis=0)
                gain = np.where(live[q, g, Q], gain, 0); m = np.argmax(gain, axis=1); ok = np.any(gain > 0, axis=1)
                Q = Q[ok]; m = m[ok]; u, i = np.unique(tg[g, Q], return_index=True)
                mov[q, g, u] = po[q, g, Q[i], m[i]]
        for r in range(N):
            win = mov[r, :, r * S:(r + 1) * S].copy()
            for o, q in enumerate([a for a in range(N) if a != r]):
                c = mov[q, :, r * S:(r + 1) * S]; e = R0 + ((N - 1) * t + o) * S
                x[r, :, :, e:e + S] = np.where((c >= 0)[:, None, :], np.take_along_axis(x[q], np.maximum(c, 0)[:, None, :], 2), 0)
                gg, kk = np.nonzero(c >= 0); home[q, gg, c[gg, kk]] = 65535
                win = np.where((win < 0) & (c >= 0), e + np.arange(S), win)
            gg, kk = np.nonzero(win >= 0); m = row[r, gg, kk]
            home[r, gg, win[gg, kk]] = 16 * (new + kk) + m; po[r, gg, new + kk, m] = win[gg, kk]
    hh = np.stack([home >> 8, home & 255], axis=2)
    ya = np.concatenate([x[..., R0:], hh[..., R0:].astype(np.int32)], axis=2).reshape(N, 128, R - R0)
    return {"ypost": np.ascontiguousarray(po.transpose(0, 1, 3, 2)).reshape(N, 128, P).astype(np.float32),
            "yh": hh[..., :R0].reshape(N, 16, R0).astype(np.float32).astype(BF), "ya": ya.astype(np.float32).astype(BF)}

@@ -1,0 +1,730 @@
+from concourse.bass import DstId, RemoteDMATransfer
+from concourse.mybir import AluOpType as Op, AxisListType as Ax, ActivationFunctionType as Fn
+
+R0, P0, SP, RO = 6144, 416, 32, 3
+R = R0 + 96 * RO
+PD = 512
+MD = 544
+WP = 672
+XW = 16 * WP
+TS = 544
+BIG = 262144.0
+SU1, SU2 = 13, 13
+HQ = 256
+SQ = [(208, 96), (224, 96), (240, 96)]
+AB = [128, 192, 64]
+
+SCRATCH = {}
+ALIAS = {}
+OWN = ("plr", "pls", "bw", "bs", "mf", "arr", "p0", "p1", "p2", "p3", "p4", "p5", "p6", "p7")
+
+
+def _b(names, w, dt="bfloat16", where="sbuf"):
+    for name in names.split():
+        if w > 100 or name.startswith(OWN):
+            SCRATCH[name] = (where, [128, w], dt)
+        else:
+            pool = "small_" + dt
+            o = SCRATCH.get(pool, ("", [0, 0]))[1][1]
+            ALIAS[name] = (pool, o, w)
+            SCRATCH[pool] = ("sbuf", [128, o + (w + 15) // 16 * 16], dt)
+
+
+F, I, U = "float32", "int32", "uint16"
+_b("x1 x2", R)
+_b("hh", R + 512)
+_b("xd", R0)
+_b("xg", XW)
+_b("ng mc md", 16 * 480)
+_b("e16 rmp rx nm hm vnm", 2048)
+_b("e16f", 2048, F)
+_b("postI nearI nsh", P0, I)
+_b("abI", 1152, I)
+_b("ab16", 1152, U)
+_b("post16 near16", 512, U)
+_b("postf nearf", WP, F)
+_b("slot", P0, F)
+_b("ctr live", WP)
+for _t in range(RO):
+    _b("tab%d" % _t, 4 * TS)
+    _b("plr%d" % _t, 6, U)
+    _b("pls%d" % _t, 2, U)
+    _b("bw%d" % _t, 144)
+    _b("bs%d" % _t, 32)
+    _b("mf%d" % _t, 128)
+    _b("arr%d" % _t, 96)
+    _b("atab%d" % _t, 96, F)
+    _b("vst%d" % _t, 512)
+_b("full scan sd1 junk", TS)
+_b("cmpv", TS + 2)
+_b("cidx", TS, F)
+_b("ident nid ibig bo bo14c bo14b bo14p bo14n px mw mw15 one0 lga u128 w128 w128b vm oh lgt lut dat", 128)
+_b("bof zx pg pgm", 128, F)
+_b("lg", 1024)
+_b("ones n15 ck cka ckb wt tq ff xs xs2 ma mb vhi vlo", 512)
+_b("bt", 480)
+_b("kt k1", 256, F)
+_b("k2", 128, F)
+_b("k3", 64, F)
+_b("fc", 64, F)
+_b("km kmf i32k dg tr whi postp nearp laf lbf ktk spa spb ownv ra wv wb wd hd fo", 32, F)
+_b("kmi kma wi wr", 32, I)
+_b("k16 lp oa obt ob go nog rw rwf wf ac lpn hw z32", 32)
+_b("g8 rgp rgn", 8)
+_b("miw", 16)
+_b("pcol pr", 2, I)
+_b("i16 r16", 16, F)
+_b("i8 cs ms", 8, F)
+_b("acc lac_f lbc_f kmx", 2, F)
+_b("pl16 lac lbc", 2, U)
+_b("la16 ps16 lb16 spl16 tgl", 32, U)
+_b("ls16 lq16 lm16 rl16", 8, U)
+_b("lsi lqi lmi", 8, I)
+_b("fa eq", 96, F)
+_b("ya1 ya2 ya3", 288)
+for _i in range(8):
+    _b("p%d" % _i, 512, F, "psum")
+
+NDMA = 16
+SEMAPHORES = ["qv", "qs", "qp", "qg", "sent"] + ["d%d" % i for i in range(NDMA)] + \
+    ["%s%d" % (a, t) for a in ("rp", "rb", "rm") for t in range(RO)]
+
+
+def rank_program(g, core, T, topo):
+    r = T.rank_of(core)
+    if r is None:
+        return
+    Q = {"v": g.vector, "s": g.scalar, "p": g.tensor, "g": g, "y": g.sync}
+    cnt = {"qv": 0, "qs": 0, "qp": 0, "qg": 0}
+    total = {}
+    known = {q: {} for q in Q}
+    acc = {}
+    dn = [0]
+
+    def waits(q, toks):
+        need = {}
+        for (sem, val, q2, snap) in toks:
+            if known[q].get(sem, 0) < val and (sem not in need or need[sem][1] < val):
+                need[sem] = (sem, val, q2, snap)
+        lst = list(need.values())
+        for tk in lst:
+            if any(o is not tk and o[3].get(tk[0], 0) >= tk[1] for o in lst):
+                continue
+            Q[q].wait_ge(T.sem[tk[0]], tk[1])
+        for tk in lst:
+            k = known[q]
+            k[tk[0]] = max(k.get(tk[0], 0), tk[1])
+            for s2, v2 in tk[3].items():
+                if k.get(s2, 0) < v2:
+                    k[s2] = v2
+
+    def deps(q, reads, writes):
+        toks = []
+        for is_w, regs in ((False, reads), (True, writes)):
+            for (b, c0, c1) in regs:
+                ps = SCRATCH.get(b, ("",))[0] == "psum"
+                for (d0, d1, w2, tok) in acc.get(b, ()):
+                    if ps:
+                        if tok[2] == q and (q == "p" or not (is_w or w2)):
+                            continue
+                        toks.append(tok)
+                    elif d0 < c1 and c0 < d1 and (is_w or w2):
+                        toks.append(tok)
+        return toks
+
+    def note(reads, writes, tok):
+        for (b, c0, c1) in writes:
+            ps = SCRATCH.get(b, ("",))[0] == "psum"
+            old = acc.get(b, [])
+            acc[b] = [o for o in old if not (ps or (c0 <= o[0] and o[1] <= c1))] + [(c0, c1, True, tok)]
+        for (b, c0, c1) in reads:
+            old = acc.get(b, [])
+            acc[b] = [o for o in old if not (not o[2] and o[3][2] == tok[2] and o[3][0] == tok[0] and c0 <= o[0] and o[1] <= c1)] + [(c0, c1, False, tok)]
+
+    def run(q, fn, reads, writes):
+        waits(q, deps(q, reads, writes))
+        sem = "q" + q
+        cnt[sem] += 1
+        total[sem] = cnt[sem]
+        fn().then_inc(T.sem[sem], 1)
+        note(reads, writes, (sem, cnt[sem], q, dict(known[q])))
+
+    def dma(q, out, in_):
+        waits(q, deps(q, in_[1], out[1]))
+        sem = "d%d" % dn[0]
+        dn[0] += 1
+        Q[q].dma_start(out[0], in_[0]).then_inc(T.sem[sem], 16)
+        total[sem] = 16
+        note(in_[1], out[1], (sem, 16, "dma", dict(known[q])))
+
+    def v(b, c0=0, c1=None, s=1):
+        if b in ALIAS:
+            b, o, w = ALIAS[b]
+            c0, c1 = o + c0, o + (w if c1 is None else c1)
+        c1 = SCRATCH[b][1][1] if c1 is None else c1
+        return (T[b][:, c0:c1] if s == 1 else T[b][:, c0:c1:s], [(b, c0, c1)])
+
+    def part(b, n, c0, c1, s):
+        return (T[b][0:n, c0:c1] if s == 1 else T[b][0:n, c0:c1:s], [(b, c0, c1)])
+
+    def ind(win, off):
+        return (win[0].indirect(off[0]), win[1] + off[1])
+
+    def col(i):
+        return v("fc", i, i + 1)
+
+    def fam(b, m):
+        return v(b, 128 * m, 128 * m + 128)
+
+    def tt(out, a, b, op):
+        run("v", lambda: g.vector.tensor_tensor(out[0], a[0], b[0], op), a[1] + b[1], out[1])
+
+    def ts(out, a, s1, o1, s2=None, o2=None):
+        regs = list(a[1])
+        x1, x2 = s1, s2
+        if isinstance(s1, tuple):
+            regs += s1[1]
+            x1 = s1[0]
+        if isinstance(s2, tuple):
+            regs += s2[1]
+            x2 = s2[0]
+        if o2 is None:
+            run("v", lambda: g.vector.tensor_scalar(out[0], a[0], x1, None, o1), regs, out[1])
+        else:
+            run("v", lambda: g.vector.tensor_scalar(out[0], a[0], x1, x2, o1, o2), regs, out[1])
+
+    def cp(out, a):
+        run("v", lambda: g.vector.tensor_copy(out[0], a[0]), a[1], out[1])
+
+    def scat(win, off, a):
+        run("v", lambda: g.vector.tensor_copy(win[0].indirect(off[0]), a[0]), a[1] + off[1] + win[1], win[1])
+
+    def red(out, a, op, ab=False):
+        kw = {"apply_absolute_value": True} if ab else {}
+        run("v", lambda: g.vector.tensor_reduce(out[0], a[0], Ax.X, op, **kw), a[1], out[1])
+
+    def tr(out, a):
+        run("v", lambda: g.vector.transpose(out[0], a[0]), a[1], out[1])
+
+    def fill(out, c):
+        run("v", lambda: g.vector.memset(out[0], c), [], out[1])
+
+    def act(out, a, fn=Fn.Copy, bias=None, scale=None, accum=None):
+        kw = {}
+        regs = list(a[1])
+        w = list(out[1])
+        if bias is not None:
+            kw["bias"] = bias[0]
+            regs += bias[1]
+        if isinstance(scale, tuple):
+            kw["scale"] = scale[0]
+            regs += scale[1]
+        elif scale is not None:
+            kw["scale"] = scale
+        if accum is not None:
+            kw["accum_out"] = accum[0]
+            w += accum[1]
+        run("s", lambda: g.scalar.activation(out[0], a[0], fn, **kw), regs, w)
+
+    def mm(out, lhsT, rhs, start, stop):
+        run("p", lambda: g.tensor.matmul(out[0], lhsT[0], rhs[0], start, stop), lhsT[1] + rhs[1], out[1])
+
+    def iota(out, pat, base=0, cm=0, flag=True):
+        kw = {"allow_small_or_imprecise_dtypes": True} if flag else {}
+        run("g", lambda: g.iota(out[0], pat, base, cm, **kw), [], out[1])
+
+    others = [q for q in range(len(T.cores)) if q != r]
+    NE = 2
+
+    def send(bufs, dsts, sem):
+        trs = []
+        regs = []
+        for i, q in enumerate(others):
+            dst = T.cores[q]
+            rid, pid, _ = topo.addr(dst)
+            eng = topo.engines(core, dst)[NE * i:NE * i + NE]
+            trs.append(RemoteDMATransfer(dst_ids=[DstId(rid=rid, pnc=pid)], dma_engine_mask=sum(1 << e for e in eng),
+                                         remote_sem=T.sem[sem], srcs=[bufs[i][0]], dsts=[dsts[i][0]]))
+            regs += bufs[i][1]
+        waits("g", deps("g", regs, []))
+        g.remote_dma_fused(trs, local_sem=T.sem["sent"])
+        total["sent"] = total.get("sent", 0) + NE * len(others)
+
+    def arrives(regs, sem):
+        n = NE * len(others)
+        total[sem] = n
+        note([], regs, (sem, n, "remote", {}))
+
+    def place(q):
+        return r - (1 if r > q else 0)
+
+    half = R0 // 2
+    dma("y", v("postI"), (T.post[:, :], []))
+    dma("s", v("hh", 0, half), (T.rec[:, 0:half], []))
+    dma("y", v("hh", half, R0), (T.rec[:, half:R0], []))
+    dma("s", v("abI"), (T.absorb[:, :], []))
+    dma("y", v("nearI"), (T.near[:, :], []))
+    dma("s", v("xd", 0, half), (T.rec[:, 0:half], []))
+    dma("y", v("xd", half, R0), (T.rec[:, half:R0], []))
+    dma("y", v("ctr", 0, P0), (T.cen[:, :], []))
+
+    pI, p15 = v("pcol", 0, 1), v("pcol", 1, 2)
+    NI = v("vnm", 0, 128)
+    R1 = v("md", 0, 2048)
+    iota(pI, [[0, 1]], 0, 1, False)
+    iota(v("vnm"), [[-1, 16], [1, 128]])
+    iota(v("i32k"), [[16, 32]])
+    iota(v("w128"), [[-1, 128]], 128)
+    iota(v("slot"), [[16, P0]])
+    iota(v("whi"), [[8, 4], [0, 8]])
+    iota(v("n15"), [[0, 32], [1, 16]])
+    iota(v("i16"), [[1, 16]])
+    iota(v("i8"), [[16, 8]])
+    iota(v("cidx"), [[1, TS]])
+    iota(v("dg"), [[0, 2], [1, 16]])
+    iota(v("postf", MD, WP), [[1, 128]], R)
+    iota(v("postf", PD, MD), [[0, 32]])
+    iota(v("tab0"), [[0, 4 * TS]])
+    fill(v("hh", R0, R), 0.0)
+    fill(v("xg", 16 * P0, XW), -1.0)
+    fill(v("live", P0, WP), 0.0)
+    fill(v("full", P0, TS), 0.0)
+    fill(v("cmpv", TS, TS + 2), -544.0)
+    fill(v("ctr", P0, WP), 0.0)
+    fill(v("nearf", P0, WP), 0.0)
+    fill(v("wt"), 0.0)
+    fill(v("ff", P0, 512), 0.0)
+    fill(v("ones"), 1.0)
+    fill(R1, -256.0)
+    fill(v("z32"), 0.0)
+    PF, MF_, PB = col(0), col(1), col(2)
+    ts(p15, pI, 15, Op.bitwise_and)
+    cp(PF, pI)
+    cp(MF_, p15)
+    tt(PB, PF, MF_, Op.subtract)
+    for i in range(7):
+        ts(col(8 + i), MF_, float(i), Op.is_equal)
+    C14, C15, N14, CF = col(16), col(17), col(18), col(19)
+    ts(C14, MF_, 14.0, Op.is_equal)
+    ts(C15, MF_, 15.0, Op.is_equal)
+    ts(CF, MF_, 13.5, Op.is_le)
+    ts(N14, MF_, 13.5, Op.is_gt)
+    ts(col(20), C14, 256.0, Op.mult, C15, Op.add)
+    K32, KN32, KN16, K16c = col(21), col(22), col(23), col(24)
+    ts(K32, CF, 32.0, Op.mult)
+    ts(KN32, CF, -32.0, Op.mult)
+    ts(KN16, CF, -16.0, Op.mult)
+    ts(K16c, CF, 16.0, Op.mult)
+    HB, HB1 = col(26), col(27)
+    ts(HB, MF_, 0.5, Op.add)
+    ts(HB1, MF_, 16.5, Op.add)
+    ts(v("e16"), v("vnm"), PB, Op.is_equal)
+    ts(v("hm"), v("e16"), col(20), Op.mult)
+    cp(v("post16", 0, P0), v("postI"))
+
+    X = v("hh", 0, R)
+    act(v("xg", 0, 16 * HQ), ind(X, v("post16", 0, HQ)))
+    ts(v("u128"), NI, PB, Op.subtract)
+    ts(v("px"), v("u128"), 0.0, Op.is_ge)
+    ts(v("w128b"), v("u128"), 15.5, Op.is_le)
+    tt(v("bo"), v("px"), v("w128b"), Op.mult)
+    ts(v("slot"), v("slot"), MF_, Op.add)
+    cp(v("postf", 0, P0), v("postI"))
+    cp(v("xg", 16 * HQ, 16 * P0), ind(X, v("post16", HQ, P0)))
+    home_parts = ((0, HQ, "p5"), (HQ, P0, "p2"))
+    for (a, b, pb) in home_parts:
+        for m in range(16):
+            mm(v(pb, a, b), fam("hm", m), v("xg", 16 * a + m, 16 * b, 16), m == 0, m == 15)
+    ts(col(28), MF_, 512.0, Op.add)
+    ts(col(29), MF_, 528.0, Op.add)
+    ts(v("scan"), v("cidx"), col(28), Op.is_ge, 16.0, Op.mult)
+    ts(v("sd1"), v("cidx"), col(29), Op.is_ge, 84.0, Op.mult)
+    tt(v("sd1"), v("sd1"), v("scan"), Op.add)
+    ts(v("ident"), NI, PF, Op.is_equal)
+    ts(v("ibig"), v("ident"), BIG, Op.mult)
+    ts(v("nid"), v("ident"), -1.0, Op.mult)
+    ts(v("w128b"), NI, PF, Op.is_gt, -32.0, Op.mult)
+    tt(v("w128b"), v("w128b"), v("bo"), Op.mult)
+    tt(v("px"), v("w128b"), v("ident"), Op.add)
+    ts(v("mw"), v("bo"), MF_, Op.mult)
+    ts(col(30), PF, 0.0, Op.is_equal)
+    ts(col(31), PF, 1.0, Op.is_equal)
+    ts(col(32), col(30), -BIG, Op.mult)
+    ts(v("one0"), NI, 0.0, Op.mult, col(30), Op.add)
+    cp(v("k16"), v("i32k"))
+    ts(v("dat"), v("w128"), col(8), Op.mult, col(9), Op.add)
+    ts(v("ckb"), v("n15"), -1.0, Op.mult, 15.0, Op.add)
+    ts(v("ckb"), v("ckb"), col(31), Op.mult)
+    ts(v("cka"), v("n15"), 0.0, Op.mult, col(32), Op.add)
+    ts(v("ck"), v("ckb"), col(32), Op.add)
+    ts(v("dg"), v("dg"), MF_, Op.is_equal)
+    for (a, b, pb) in home_parts:
+        tt(v("live", a, b), v("slot", a, b), v(pb, a, b), Op.is_equal)
+
+    def constants_b():
+        ts(v("nsh"), v("nearI"), 9, Op.arith_shift_right)
+        ts(v("nsh"), v("nsh"), 32, Op.mult)
+        tt(v("nearf", 0, P0), v("nsh"), v("nearI"), Op.add)
+        cp(v("near16", 0, P0), v("nearf", 0, P0))
+        cp(v("ab16"), v("abI"))
+        act(v("rx"), v("e16"), scale=KN16)
+        act(v("rmp"), v("e16"), scale=K32)
+        act(v("nm"), v("e16"), scale=col(8))
+        run("g", lambda: g.affine_select(R1[0], R1[0], [[-1, 16], [1, 128]], Op.is_gt, 0.0, 1, -1), R1[1], R1[1])
+        run("g", lambda: g.affine_select(R1[0], R1[0], [[0, 16], [-1, 128]], Op.is_gt, 0.0, 15, 1), R1[1], R1[1])
+        dma("y", (T["nm"][1:128:16, :], [("nm", 0, 2048)]), (T["md"][1:128:16, 0:2048], R1[1]))
+
+    def constants_c():
+        ts(v("g8"), v("i8"), PB, Op.is_equal)
+        ts(v("rgp"), v("g8"), K32, Op.mult)
+        ts(v("rgn"), v("g8"), KN32, Op.mult)
+        ts(v("bo14p"), v("bo"), K16c, Op.mult)
+        ts(v("bo14n"), v("bo"), KN16, Op.mult)
+        ts(v("u128"), v("n15", 0, 128), SU1 - 0.5, Op.is_ge, -2.0, Op.mult)
+        ts(v("u128"), v("u128"), 1.0, Op.add)
+        tt(v("bo14c"), v("u128"), v("bo14n"), Op.mult)
+        ts(v("u128"), v("n15", 0, 128), SU2 - 0.5, Op.is_ge, -2.0, Op.mult)
+        ts(v("u128"), v("u128"), 1.0, Op.add)
+        tt(v("bo14b"), v("u128"), v("bo14p"), Op.mult)
+        A, B = col(33), col(34)
+        ts(A, col(12), 32768.0, Op.mult)
+        ts(A, col(14), 16.0, Op.mult, A, Op.add)
+        ts(B, col(8), 32768.0, Op.mult, col(9), Op.add)
+        for (i, w) in ((10, -256.0), (11, -16.0), (12, -32768.0 * 128), (13, -15.0)):
+            ts(B, col(i), w, Op.mult, B, Op.add)
+        ts(v("lga"), NI, A, Op.mult, B, Op.add)
+        for k in range(8):
+            ts(col(40 + k), PB, 16.0 * k, Op.is_equal)
+        for k in range(8):
+            ts(v("lg", 128 * k, 128 * k + 128), v("lga"), col(40 + k), Op.mult)
+        ts(v("pr", 0, 1), pI, 4, Op.arith_shift_right)
+        cp(col(35), v("pr", 0, 1))
+        ts(v("wt", 2, 512, 16), v("whi"), col(35), Op.add)
+        ts(v("wt", 3, 512, 16), v("whi"), 0.0, Op.mult, MF_, Op.add)
+        for k in (4, 5):
+            ts(v("wt", k, 512, 16), v("whi"), 0.0, Op.mult, 1.0, Op.add)
+        ts(col(36), col(10), -34.0, Op.mult, col(14), Op.add)
+        cp(v("tq", 31, 32), col(36))
+        ts(v("r16"), v("i16"), MF_, Op.is_equal)
+        ts(v("cs"), v("i8"), PB, Op.is_equal)
+        ts(v("miw"), v("i16"), MF_, Op.is_equal)
+
+    def constants_d():
+        act(v("e16f"), v("e16"))
+        iota(v("vhi"), [[1, 2], [0, 256]], 26)
+        iota(v("vlo"), [[0, 2], [1, 256]])
+        for k in range(RO):
+            iota(v("atab%d" % k), [[32 - 8192, 3], [1, 32]], 3 * 8192 + R0 + 96 * k)
+        for k in range(1, RO):
+            iota(v("tab%d" % k), [[0, 4 * TS]])
+        ts(v("w128b"), v("n15", 0, 128), 15.0, Op.is_equal)
+        tt(v("mw15"), v("mw"), v("w128b"), Op.mult)
+        cp(v("bof"), v("bo"))
+        ts(v("tr"), v("i32k"), MF_, Op.add, float(R), Op.add)
+        fill(v("vm"), 255.0)
+        ts(v("vst0"), v("vhi"), C14, Op.mult)
+        ts(v("vlo"), v("vlo"), C15, Op.mult)
+        tt(v("vst0"), v("vst0"), v("vlo"), Op.add)
+        for t in range(1, RO):
+            ts(col(36 + t), C14, 2.0 * t, Op.mult)
+            ts(v("vst%d" % t), v("vst0"), col(36 + t), Op.add)
+
+    deferred = []
+
+    for t in range(RO):
+        nq = P0 + SP * t
+        nc = nq // 16
+        last = t == RO - 1
+        xa = ["hh", "x1", "x2"][t]
+        xb = ["x1", "x2", "x1"][t]
+        Xa = v(xa, 0, R)
+        Xb = v(xb, 0, R)
+        tab, plr, pls, bw, bs, mf, arr = [n + str(t) for n in ("tab", "plr", "pls", "bw", "bs", "mf", "arr")]
+        p0 = lambda a=0, b=512: v("p0", a, b)
+        p1 = lambda a=0, b=512: v("p1", a, b)
+
+        mm(p0(0, nq), v("bo"), v("live", 0, nq), True, True)
+        ts(v("full", 0, nq), p0(0, nq), 13.5, Op.is_ge)
+        run("v", lambda: g.vector.tensor_tensor_scan(v("scan")[0], v("full")[0], v("sd1")[0], 0.0, Op.add, Op.max),
+            v("full")[1] + v("sd1")[1], v("scan")[1])
+        act(v("junk"), v("scan"), Fn.Sign, bias=HB, scale=-1.0, accum=v("acc", 0, 1))
+        ts(v("cmpv", 0, TS), v("scan"), HB1, Op.is_le, 2.0, Op.mult)
+        red(v("acc", 1, 2), v("cmpv", 0, TS + 1), Op.add)
+        ts(v(pls), v("acc"), 0.5, Op.mult, 272.0 + TS * r, Op.add)
+        send([v(pls)] * 3, [v("plr%d" % t, 2 * place(q), 2 * place(q) + 2) for q in others], "rp%d" % t)
+        arrives([(plr, 0, 6)], "rp%d" % t)
+        if t > 0:
+            deferred[0]()
+        ts(v("pl16"), v("acc"), 0.5, Op.mult, 272.0, Op.add)
+        scat(v(tab), v(pls), v("dat", 32 * r, 32 * r + 32))
+        cp(v("lp"), ind(v("live"), v("pl16")))
+        cp(v("postp"), ind(v("postf"), v("pl16")))
+        cp(v("ps16"), v("postp"))
+        mm(p1(0, 32), v("px"), v("lp"), True, True)
+        scat(v("live"), v("pl16"), v("z32"))
+        if t == 0:
+            constants_b()
+        pieces = []
+        a = 384 * t
+        o = 0
+        for w in AB:
+            pieces.append((a, a + w, 16 * o))
+            a += w
+            o += w
+
+        def absorb(i):
+            a, b, c = pieces[i]
+            w = 16 * (b - a)
+            tt(v(xb, c, c + w), ind(Xa, v("ab16", a, b)), v("xd", c, c + w), Op.max)
+
+        absorb(0)
+        act(v(xb, R0, R), v(xa, R0, R))
+        ts(v("oa"), p1(0, 32), 0.0, Op.max)
+        mm(p0(0, 32), v("mw"), v("oa"), True, False)
+        mm(p0(0, 32), v("one0"), v("k16"), False, True)
+        cp(v("la16"), p0(0, 32))
+        cp(v("laf"), p0(0, 32))
+        for (c0, c1, d0, d1) in ((0, 2 * r, 0, 32 * r), (2 * r, 6, 32 * r + 32, 128)):
+            if c1 > c0:
+                scat(v(tab), v(plr, c0, c1), v("dat", d0, d1))
+        qh = (nq // 2) // 16 * 16
+        halves = ((0, qh, "p2"), (qh, nq, "p6"))
+        for (qa, qb, pn) in halves:
+            act(v("ng", 16 * qa, 16 * qb), ind(v(tab), v("near16", qa, qb)))
+        for i in range(1, len(pieces)):
+            absorb(i)
+        XS = v("xs")
+        cp(XS, ind(Xb, v("ps16")))
+        cp(v("xs2"), XS)
+        tt(v("ma"), ind(XS, v("la16")), v("xs2"), Op.max)
+        sq, v1 = SQ[t]
+        if t > 0:
+            deferred[1]()
+        cp(v("xg", 16 * sq, 16 * (sq + v1)), ind(Xb, v("post16", sq, sq + v1)))
+        mm(p1(0, 32), v("ck", 0, 128), v("ones", 0, 32), True, False)
+        mm(p1(0, 32), v("ibig"), v("lp"), False, False)
+        for m in range(16):
+            mm(p1(0, 32), fam("rx", m), v("xs", m, 512, 16), False, False)
+        for m in range(16):
+            mm(p1(0, 32), fam("rmp", m), v("ma", m, 512, 16), False, m == 15)
+        tr(v("ktk"), p1(0, 32))
+        for h in range(2):
+            red(v("kmx", h, h + 1), v("ktk", 16 * h, 16 * h + 16), Op.max)
+        for h in range(2):
+            ts(v("obt", 16 * h, 16 * h + 16), v("ktk", 16 * h, 16 * h + 16), v("kmx", h, h + 1), Op.is_equal)
+        tr(v("ob"), v("obt"))
+        mm(p0(0, 32), v("mw"), v("ob"), True, False)
+        mm(p0(0, 32), v("one0"), v("k16"), False, True)
+        tt(v("lbf"), v("dg"), p0(0, 32), Op.mult)
+        for h in range(2):
+            red(v("lbc_f", h, h + 1), v("lbf", 16 * h, 16 * h + 16), Op.add)
+        cp(v("lbc"), v("lbc_f"))
+        cp(v(bs), ind(XS, v("lbc")))
+        send([v(bs)] * 3, [v("bw%d" % t, 32 * r, 32 * r + 32)] * 3, "rb%d" % t)
+        if not last:
+            dma("y", v("xd"), v(xb, 0, R0))
+        cp(v("lb16"), p0(0, 32))
+        cp(v(bw, 32 * r, 32 * r + 32), v(bs))
+        fill(v(bw, 128, 144), 8192.0)
+        for q in others:
+            arrives([(bw, 32 * q, 32 * q + 32)], "rb%d" % t)
+
+        if t == 0:
+            act(v("hm"), v("e16"), scale=KN32)
+        act(v("xg", 0, 16 * sq), ind(Xb, v("post16", 0, sq)))
+        for (qa, qb, pn) in halves:
+            for j in range(16):
+                mm(v(pn, qa, qb), fam("nm", j), v("ng", 16 * qa + j, 16 * qb, 16), j == 0, j == 15)
+            act(v("ff", qa, qb), v(pn, qa, qb), Fn.Relu)
+        cp(v("xg", 16 * (sq + v1), 16 * nq), ind(Xb, v("post16", sq + v1, nq)))
+        if t == 0:
+            constants_c()
+        for k in range(16):
+            mm(p0(0, nc), fam("e16", k), v("ff", k, nq, 16), k == 0, k == 15)
+        for c in range(4):
+            mm(v("p2", 8 * c, 8 * c + 8), v("ff", 128 * c, 128 * c + 128), v("g8"), True, True)
+        mm(v("p3", 0, nq), v("ident"), v("ctr", 0, nq), True, True)
+        ts(v("tgl", 0, nc), p0(0, nc), -1.0, Op.mult, 128.0, Op.add)
+
+        chunks = [(c, min(nq, 128 * c + 128) - 128 * c) for c in range(4)]
+        mm(v("p5"), v("ones", 0, 128), v("cka"), True, False)
+        for c in range(4):
+            gc = v("p5", 128 * c, 128 * c + 128)
+            mm(gc, v("live", 128 * c, 128 * c + 128), v("ibig"), False, False)
+            mm(gc, v("ctr", 128 * c, 128 * c + 128), v("bo14c"), False, False)
+        flip = [0]
+        pend = []
+
+        def xm(m):
+            return v("xg", m, 16 * nq, 16)
+
+        def s_unit(m, other, dst, sums):
+            pb = "p6" if flip[0] % 2 else "p7"
+            flip[0] += 1
+            mm(v(pb, 0, nq), v("ident"), xm(m), True, False)
+            mm(v(pb, 0, nq), v("nid"), other, False, True)
+            act(v(dst, m * 480, m * 480 + nq), v(pb, 0, nq), Fn.Relu)
+            return (sums, m, dst)
+
+        def add(u):
+            sums, m, dst = u
+            for c, n in chunks:
+                mm(part("p5", n, 128 * c + m, 128 * c + 128, 16), v(dst, m * 480 + 128 * c, m * 480 + 128 * c + n), v(sums), False, False)
+
+        def pipe(u):
+            pend.append(u)
+            if len(pend) > 2:
+                add(pend.pop(0))
+
+        def distances(other_sb, other_ps, dst, sums, su):
+            vm_ = list(range(su))
+            sm_ = list(range(su, 16))
+            while vm_ or sm_:
+                if sm_ and (not vm_ or len(sm_) * su >= len(vm_) * (16 - su)):
+                    pipe(s_unit(sm_.pop(0), other_sb, dst, sums))
+                else:
+                    m = vm_.pop(0)
+                    tt(v(dst, m * 480, m * 480 + nq), xm(m), other_ps, Op.max)
+                    pipe((sums, m, dst))
+
+        distances(v("ctr", 0, nq), v("p3", 0, nq), "mc", "rgp", SU1)
+        act(v("bt", 0, nq), ind(v(bw, 0, 144), v("tgl", 0, nc)))
+        mm(v("p4", 0, nq), v("ident"), v("bt", 0, nq), True, True)
+        for c, n in chunks:
+            mm(part("p5", n, 128 * c, 128 * c + 128, 1), v("bt", 128 * c, 128 * c + n), v("bo14b"), False, False)
+        distances(v("bt", 0, nq), v("p4", 0, nq), "md", "rgn", SU2)
+        while pend:
+            add(pend.pop(0))
+        mm(v("p5"), v("ones", 0, 128), v("ckb"), False, True)
+
+        cp(v("kt"), v("p5", 1, 512, 2))
+        tt(v("k1"), v("p5", 0, 512, 2), v("kt"), Op.max)
+        prev, w = "k1", 256
+        for nxt in ("k2", "k3", "km"):
+            w //= 2
+            tt(v(nxt), v(prev, 0, 2 * w, 2), v(prev, 1, 2 * w, 2), Op.max)
+            prev = nxt
+        cp(v("kmi"), v("km"))
+        ts(v("kmf"), v("km"), 15.5, Op.is_ge)
+        ts(v("kma"), v("kmi"), 15, Op.bitwise_and)
+        tt(v("wt", 0, 512, 16), v("kmf"), v("p2", 0, 32), Op.mult)
+        cp(v("wt", 1, 512, 16), v("kma"))
+        for c in range(4):
+            mm(v("p%d" % (c // 2), 128 * (c % 2), 128 * (c % 2) + 128), v("wt", 128 * c, 128 * c + 128), v("ident"), True, True)
+        cp(v("tq", 32, 288), v("p0", 0, 256))
+        act(v("tq", 288, 32 + nq), v("p1", 0, nq - 256))
+        banks = ["p3", "p4", "p2", "p6", "p7", "p0", "p1", "p5"]
+        for k in range(8):
+            mm(v(banks[k], 0, nq + 1), v("lg", 128 * k, 128 * k + 128), v("tq", 31, 32 + nq), True, True)
+        for k in range(8):
+            red(v("ms", k, k + 1), v(banks[k], 0, nq + 1), Op.min, True)
+            act(v("zx", 16 * k, 16 * k + 16), v("r16"), scale=v("ms", k, k + 1))
+        mm(p0(0, 8), v("zx"), v("cs"), True, True)
+        cp(v("ls16"), p0(0, 8))
+        cp(v(mf), ind(v("xg"), v("ls16")))
+        send([v(mf, 32 * q, 32 * q + 32) for q in others],
+             [v("arr%d" % t, 32 * place(q), 32 * place(q) + 32) for q in others], "rm%d" % t)
+        arrives([(arr, 0, 96)], "rm%d" % t)
+
+        tt(v("mb"), ind(XS, v("lb16")), v("xs2"), Op.max)
+        cp(v("lsi"), p0(0, 8))
+        ts(v("lqi"), v("lsi"), 4, Op.arith_shift_right)
+        ts(v("lmi"), v("lsi"), 15, Op.bitwise_and)
+        cp(v("lq16"), v("lqi"))
+        cp(v("lm16"), v("lmi"))
+        if t == 0:
+            constants_d()
+        tt(v("laf"), v("laf"), v("dg"), Op.mult)
+        for h in range(2):
+            red(v("lac_f", h, h + 1), v("laf", 16 * h, 16 * h + 16), Op.add)
+        cp(v("lac"), v("lac_f"))
+        act(v("ac"), ind(XS, v("lac")))
+        if not last:
+            act(v("lgt"), ind(v("live"), v("lq16")))
+        act(v("oh"), ind(v("miw"), v("lm16")))
+        act(v("pg"), ind(v("postf"), v("lq16")))
+        mm(p1(0, 32), v("ck", 0, 128), v("ones", 0, 32), True, False)
+        mm(p1(0, 32), v("ibig"), v("lp"), False, False)
+        for m in range(16):
+            mm(p1(0, 32), fam("rmp", m), v("ma", m, 512, 16), False, False)
+        for m in range(16):
+            mm(p1(0, 32), fam("hm", m), v("mb", m, 512, 16), False, False)
+        mm(p1(0, 32), v("bo14p"), v(bs), False, False)
+        mm(p1(0, 32), v("bo14n"), v("ac"), False, True)
+        if not last:
+            tt(v("lut"), v("lgt"), v("oh"), Op.subtract)
+            scat(v("live"), v("lq16"), v("lut"))
+        ts(v("go"), p1(0, 32), 15.5, Op.is_ge)
+        ts(v("nog"), p1(0, 32), 15.5, Op.is_lt)
+        mm(p0(0, 32), v("px"), v("nog"), True, True)
+        tt(v("pgm"), v("pg"), v("oh"), Op.mult)
+        mm(v("p4", 0, 32), v("bof"), v("pgm", 32 * r, 32 * r + 32), True, True)
+        if not last:
+            tt(v("lpn"), v("lp"), v("go"), Op.subtract)
+            scat(v("live"), v("pl16"), v("lpn"))
+        ts(v("rw"), p0(0, 32), 0.0, Op.max)
+        ts(v("fo"), v(mf, 32 * r, 32 * r + 32), 0.0, Op.is_ge, 2.0 ** -17, Op.max)
+        ts(v("ra"), v("p4", 0, 32), 32768.0, Op.add)
+        tt(v("ownv"), v("ra"), v("fo"), Op.mult)
+        mm(v("p7", 0, 32), v("mw15"), v("rw"), True, True)
+        for k in range(16):
+            mm(v("p6", 0, 8), fam("e16f", k), v("pgm", k, 128, 16), k == 0, k == 15)
+
+        ts(v("eq"), v(arr), 0.0, Op.is_ge)
+        tt(v("fa"), v("eq"), v("atab%d" % t), Op.mult)
+        tt(v("wv"), v("fa", 0, 32), v("ownv"), Op.max)
+        tt(v("wb"), v("fa", 32, 64), v("fa", 64, 96), Op.max)
+        tt(v("wv"), v("wv"), v("wb"), Op.max)
+        ts(v("wf"), v("wv"), 8191.5, Op.is_ge)
+        tt(v("rwf"), v("rw"), v("wf"), Op.mult)
+        if not last:
+            tt(v("live", nq, nq + 32), v("go"), v("rwf"), Op.add)
+        ts(v(xb, R0 + 96 * t, R0 + 96 * t + 96), v(arr), 0.0, Op.max)
+
+        def rest(t=t, nq=nq):
+            cp(v("wi"), v("wv"))
+            ts(v("wr"), v("wi"), 8191, Op.bitwise_and)
+            cp(v("wd"), v("wr"))
+            tt(v("wb"), v("wd"), v("postp"), Op.subtract)
+            tt(v("wd"), v("wb"), v("rwf"), Op.mult)
+            tt(v("postf", nq, nq + 32), v("wd"), v("postp"), Op.add)
+            if t < RO - 1:
+                cp(v("post16", nq, nq + 32), v("postf", nq, nq + 32))
+                act(v("nearp"), ind(v("nearf"), v("pl16")))
+                cp(v("near16", nq, nq + 32), v("nearp"))
+                act(v("nearf", nq, nq + 32), v("nearp"))
+                scat(v("ctr"), v("pl16"), v("ac"))
+                act(v("ctr", nq, nq + 32), v("bs%d" % t))
+            tt(v("spa"), v("postp"), v("tr"), Op.subtract)
+            tt(v("spb"), v("spa"), v("go"), Op.mult)
+            tt(v("spa"), v("spb"), v("tr"), Op.add)
+            cp(v("spl16"), v("spa"))
+
+        def homes(t=t):
+            tt(v("hw"), v("vst%d" % t, 0, 512, 16), v("p7", 0, 32), Op.add)
+            cp(v("rl16"), v("p6", 0, 8))
+            cp(v("vm", 32 * r, 32 * r + 32), v("hw"))
+            ts(v("hd"), v("hw"), -255.0, Op.add)
+            for k in range(3):
+                tt(v("eq", 32 * k, 32 * k + 32), v("fa", 32 * k, 32 * k + 32), v("wv"), Op.is_equal)
+            for k in range(3):
+                tt(v("fa", 32 * k, 32 * k + 32), v("eq", 32 * k, 32 * k + 32), v("hd"), Op.mult)
+            ts(v("hh", R0 + 96 * t, R0 + 96 * t + 96), v("fa"), 255.0, Op.add)
+            scat(v("hh"), v("spl16"), v("vst%d" % t))
+            scat(v("hh"), v("rl16"), v("vm"))
+
+        if last:
+            rest()
+            homes()
+        else:
+            deferred = [rest, homes]
+
+    dma("y", (T.ypost[:, :], []), v("postf", 0, 512))
+    dma("y", (T.yh[0:16:2, :], []), (T["hh"][14:128:16, 0:R0], [("hh", 0, R0)]))
+    dma("s", (T.yh[1:16:2, :], []), (T["hh"][15:128:16, 0:R0], [("hh", 0, R0)]))
+    ts(v("ya1"), v("x1", R0, R), CF, Op.mult)
+    ts(v("ya2"), v("hh", R0, R), N14, Op.mult)
+    tt(v("ya3"), v("ya1"), v("ya2"), Op.add)
+    dma("y", (T.ya[:, :], []), v("ya3"))
+    for sem, val in total.items():
+        g.wait_ge(T.sem[sem], val)

@@ -9,9 +9,10 @@ WP = 672
 XW = 16 * WP
 TS = 544
 BIG = 262144.0
-SU1, SU2 = 13, 13
-HQ = 256
-SQ = [(208, 96), (224, 96), (240, 96)]
+SU1, SU2 = 15, 12
+LEAD, LAG = 5, 4
+HQ = (112, 224)
+VQ = (64, 128)
 AB = [128, 192, 64]
 
 SCRATCH = {}
@@ -286,7 +287,6 @@ def rank_program(g, core, T, topo):
     iota(v("postf", PD, MD), [[0, 32]])
     iota(v("tab0"), [[0, 4 * TS]])
     fill(v("hh", R0, R), 0.0)
-    fill(v("xg", 16 * P0, XW), -1.0)
     fill(v("live", P0, WP), 0.0)
     fill(v("full", P0, TS), 0.0)
     fill(v("cmpv", TS, TS + 2), -544.0)
@@ -295,7 +295,6 @@ def rank_program(g, core, T, topo):
     fill(v("wt"), 0.0)
     fill(v("ff", P0, 512), 0.0)
     fill(v("ones"), 1.0)
-    fill(R1, -256.0)
     fill(v("z32"), 0.0)
     PF, MF_, PB = col(0), col(1), col(2)
     ts(p15, pI, 15, Op.bitwise_and)
@@ -319,20 +318,39 @@ def rank_program(g, core, T, topo):
     ts(HB, MF_, 0.5, Op.add)
     ts(HB1, MF_, 16.5, Op.add)
     ts(v("e16"), v("vnm"), PB, Op.is_equal)
-    ts(v("hm"), v("e16"), col(20), Op.mult)
+    act(v("hm"), v("e16"), scale=col(20))
     cp(v("post16", 0, P0), v("postI"))
 
     X = v("hh", 0, R)
-    act(v("xg", 0, 16 * HQ), ind(X, v("post16", 0, HQ)))
+    ts(col(37), PF, 0.0, Op.mult, -256.0, Op.add)
+    act(v("slot"), v("slot"), Fn.Identity, bias=MF_)
+    act(R1, v("e16"), Fn.Identity, scale=0.0, bias=col(37))
+    home_parts = ((0, HQ[0], "p5"), (HQ[0], HQ[1], "p2"), (HQ[1], P0, "p6"))
+    for (a, b, pb) in home_parts[0:2]:
+        act(v("xg", 16 * a, 16 * b), ind(X, v("post16", a, b)))
     ts(v("u128"), NI, PB, Op.subtract)
     ts(v("px"), v("u128"), 0.0, Op.is_ge)
     ts(v("w128b"), v("u128"), 15.5, Op.is_le)
     tt(v("bo"), v("px"), v("w128b"), Op.mult)
-    ts(v("slot"), v("slot"), MF_, Op.add)
     cp(v("postf", 0, P0), v("postI"))
-    cp(v("xg", 16 * HQ, 16 * P0), ind(X, v("post16", HQ, P0)))
-    home_parts = ((0, HQ, "p5"), (HQ, P0, "p2"))
-    for (a, b, pb) in home_parts:
+    ts(v("g8"), v("i8"), PB, Op.is_equal)
+    act(v("rgp"), v("g8"), scale=K32)
+    act(v("rgn"), v("g8"), scale=KN32)
+    act(v("bo14p"), v("bo"), scale=K16c)
+    act(v("bo14n"), v("bo"), scale=KN16)
+    A, B = col(33), col(34)
+    ts(A, col(12), 32768.0, Op.mult)
+    ts(A, col(14), 16.0, Op.mult, A, Op.add)
+    ts(B, col(8), 32768.0, Op.mult, col(9), Op.add)
+    for (i, w) in ((10, -256.0), (11, -16.0), (12, -32768.0 * 128), (13, -15.0)):
+        ts(B, col(i), w, Op.mult, B, Op.add)
+    ts(v("lga"), NI, A, Op.mult, B, Op.add)
+    for k in range(8):
+        ts(col(40 + k), PB, 16.0 * k, Op.is_equal)
+    for k in range(8):
+        act(v("lg", 128 * k, 128 * k + 128), v("lga"), scale=col(40 + k))
+    cp(v("xg", 16 * HQ[1], 16 * P0), ind(X, v("post16", HQ[1], P0)))
+    for (a, b, pb) in (home_parts[0], home_parts[2], home_parts[1]):
         for m in range(16):
             mm(v(pb, a, b), fam("hm", m), v("xg", 16 * a + m, 16 * b, 16), m == 0, m == 15)
     ts(col(28), MF_, 512.0, Op.add)
@@ -358,12 +376,11 @@ def rank_program(g, core, T, topo):
     ts(v("cka"), v("n15"), 0.0, Op.mult, col(32), Op.add)
     ts(v("ck"), v("ckb"), col(32), Op.add)
     ts(v("dg"), v("dg"), MF_, Op.is_equal)
-    for (a, b, pb) in home_parts:
+    for (a, b, pb) in (home_parts[0], home_parts[2], home_parts[1]):
         tt(v("live", a, b), v("slot", a, b), v(pb, a, b), Op.is_equal)
 
     def constants_b():
-        ts(v("nsh"), v("nearI"), 9, Op.arith_shift_right)
-        ts(v("nsh"), v("nsh"), 32, Op.mult)
+        ts(v("nsh"), v("nearI"), 4, Op.arith_shift_right, 96, Op.bitwise_and)
         tt(v("nearf", 0, P0), v("nsh"), v("nearI"), Op.add)
         cp(v("near16", 0, P0), v("nearf", 0, P0))
         cp(v("ab16"), v("abI"))
@@ -375,28 +392,12 @@ def rank_program(g, core, T, topo):
         dma("y", (T["nm"][1:128:16, :], [("nm", 0, 2048)]), (T["md"][1:128:16, 0:2048], R1[1]))
 
     def constants_c():
-        ts(v("g8"), v("i8"), PB, Op.is_equal)
-        ts(v("rgp"), v("g8"), K32, Op.mult)
-        ts(v("rgn"), v("g8"), KN32, Op.mult)
-        ts(v("bo14p"), v("bo"), K16c, Op.mult)
-        ts(v("bo14n"), v("bo"), KN16, Op.mult)
         ts(v("u128"), v("n15", 0, 128), SU1 - 0.5, Op.is_ge, -2.0, Op.mult)
         ts(v("u128"), v("u128"), 1.0, Op.add)
         tt(v("bo14c"), v("u128"), v("bo14n"), Op.mult)
         ts(v("u128"), v("n15", 0, 128), SU2 - 0.5, Op.is_ge, -2.0, Op.mult)
         ts(v("u128"), v("u128"), 1.0, Op.add)
         tt(v("bo14b"), v("u128"), v("bo14p"), Op.mult)
-        A, B = col(33), col(34)
-        ts(A, col(12), 32768.0, Op.mult)
-        ts(A, col(14), 16.0, Op.mult, A, Op.add)
-        ts(B, col(8), 32768.0, Op.mult, col(9), Op.add)
-        for (i, w) in ((10, -256.0), (11, -16.0), (12, -32768.0 * 128), (13, -15.0)):
-            ts(B, col(i), w, Op.mult, B, Op.add)
-        ts(v("lga"), NI, A, Op.mult, B, Op.add)
-        for k in range(8):
-            ts(col(40 + k), PB, 16.0 * k, Op.is_equal)
-        for k in range(8):
-            ts(v("lg", 128 * k, 128 * k + 128), v("lga"), col(40 + k), Op.mult)
         ts(v("pr", 0, 1), pI, 4, Op.arith_shift_right)
         cp(col(35), v("pr", 0, 1))
         ts(v("wt", 2, 512, 16), v("whi"), col(35), Op.add)
@@ -427,7 +428,7 @@ def rank_program(g, core, T, topo):
         tt(v("vst0"), v("vst0"), v("vlo"), Op.add)
         for t in range(1, RO):
             ts(col(36 + t), C14, 2.0 * t, Op.mult)
-            ts(v("vst%d" % t), v("vst0"), col(36 + t), Op.add)
+            act(v("vst%d" % t), v("vst0"), Fn.Identity, bias=col(36 + t))
 
     deferred = []
 
@@ -483,7 +484,7 @@ def rank_program(g, core, T, topo):
         mm(p0(0, 32), v("mw"), v("oa"), True, False)
         mm(p0(0, 32), v("one0"), v("k16"), False, True)
         cp(v("la16"), p0(0, 32))
-        cp(v("laf"), p0(0, 32))
+        tt(v("laf"), v("dg"), p0(0, 32), Op.mult)
         for (c0, c1, d0, d1) in ((0, 2 * r, 0, 32 * r), (2 * r, 6, 32 * r + 32, 128)):
             if c1 > c0:
                 scat(v(tab), v(plr, c0, c1), v("dat", d0, d1))
@@ -497,10 +498,7 @@ def rank_program(g, core, T, topo):
         cp(XS, ind(Xb, v("ps16")))
         cp(v("xs2"), XS)
         tt(v("ma"), ind(XS, v("la16")), v("xs2"), Op.max)
-        sq, v1 = SQ[t]
-        if t > 0:
-            deferred[1]()
-        cp(v("xg", 16 * sq, 16 * (sq + v1)), ind(Xb, v("post16", sq, sq + v1)))
+        cp(v("xg", 0, 16 * VQ[0]), ind(Xb, v("post16", 0, VQ[0])))
         mm(p1(0, 32), v("ck", 0, 128), v("ones", 0, 32), True, False)
         mm(p1(0, 32), v("ibig"), v("lp"), False, False)
         for m in range(16):
@@ -531,20 +529,19 @@ def rank_program(g, core, T, topo):
 
         if t == 0:
             act(v("hm"), v("e16"), scale=KN32)
-        act(v("xg", 0, 16 * sq), ind(Xb, v("post16", 0, sq)))
+            iota(v("xg", 16 * P0, XW), [[0, XW - 16 * P0]], -1)
+        for (a, b) in ((VQ[1], 256), (256, nq)):
+            act(v("xg", 16 * a, 16 * b), ind(Xb, v("post16", a, b)))
+        if t > 0:
+            deferred[1]()
         for (qa, qb, pn) in halves:
             for j in range(16):
                 mm(v(pn, qa, qb), fam("nm", j), v("ng", 16 * qa + j, 16 * qb, 16), j == 0, j == 15)
             act(v("ff", qa, qb), v(pn, qa, qb), Fn.Relu)
-        cp(v("xg", 16 * (sq + v1), 16 * nq), ind(Xb, v("post16", sq + v1, nq)))
+        cp(v("xg", 16 * VQ[0], 16 * VQ[1]), ind(Xb, v("post16", VQ[0], VQ[1])))
         if t == 0:
             constants_c()
-        for k in range(16):
-            mm(p0(0, nc), fam("e16", k), v("ff", k, nq, 16), k == 0, k == 15)
-        for c in range(4):
-            mm(v("p2", 8 * c, 8 * c + 8), v("ff", 128 * c, 128 * c + 128), v("g8"), True, True)
         mm(v("p3", 0, nq), v("ident"), v("ctr", 0, nq), True, True)
-        ts(v("tgl", 0, nc), p0(0, nc), -1.0, Op.mult, 128.0, Op.add)
 
         chunks = [(c, min(nq, 128 * c + 128) - 128 * c) for c in range(4)]
         mm(v("p5"), v("ones", 0, 128), v("cka"), True, False)
@@ -555,44 +552,53 @@ def rank_program(g, core, T, topo):
         flip = [0]
         pend = []
 
-        def xm(m):
-            return v("xg", m, 16 * nq, 16)
+        def xm(m, a=0, b=nq):
+            return v("xg", 16 * a + m, 16 * b, 16)
 
         def s_unit(m, other, dst, sums):
-            pb = "p6" if flip[0] % 2 else "p7"
+            pb = ("p6", "p7", "p1")[flip[0] % 3]
             flip[0] += 1
             mm(v(pb, 0, nq), v("ident"), xm(m), True, False)
             mm(v(pb, 0, nq), v("nid"), other, False, True)
             act(v(dst, m * 480, m * 480 + nq), v(pb, 0, nq), Fn.Relu)
-            return (sums, m, dst)
+            return (sums, m, dst, chunks)
 
         def add(u):
-            sums, m, dst = u
-            for c, n in chunks:
+            sums, m, dst, cs = u
+            for c, n in cs:
                 mm(part("p5", n, 128 * c + m, 128 * c + 128, 16), v(dst, m * 480 + 128 * c, m * 480 + 128 * c + n), v(sums), False, False)
 
         def pipe(u):
             pend.append(u)
-            if len(pend) > 2:
+            if len(pend) > LAG:
                 add(pend.pop(0))
 
-        def distances(other_sb, other_ps, dst, sums, su):
+        def v_unit(m, pb, dst, sums, a, b):
+            tt(v(dst, m * 480 + a, m * 480 + b), xm(m, a, b), v(pb, a, b), Op.max)
+            pipe((sums, m, dst, [x for x in chunks if a <= 128 * x[0] < b]))
+
+        def distances(other, pb, dst, sums, su, a):
             vm_ = list(range(su))
             sm_ = list(range(su, 16))
             while vm_ or sm_:
-                if sm_ and (not vm_ or len(sm_) * su >= len(vm_) * (16 - su)):
-                    pipe(s_unit(sm_.pop(0), other_sb, dst, sums))
+                if sm_ and (not vm_ or len(sm_) * su >= (len(vm_) - LEAD) * (16 - su)):
+                    pipe(s_unit(sm_.pop(0), other, dst, sums))
                 else:
-                    m = vm_.pop(0)
-                    tt(v(dst, m * 480, m * 480 + nq), xm(m), other_ps, Op.max)
-                    pipe((sums, m, dst))
+                    v_unit(vm_.pop(0), pb, dst, sums, a, nq)
 
-        distances(v("ctr", 0, nq), v("p3", 0, nq), "mc", "rgp", SU1)
+        for m in range(SU1):
+            v_unit(m, "p3", "mc", "rgp", 0, 256)
+        for k in range(16):
+            mm(p0(0, nc), fam("e16", k), v("ff", k, nq, 16), k == 0, k == 15)
+        for c in range(4):
+            mm(v("p2", 8 * c, 8 * c + 8), v("ff", 128 * c, 128 * c + 128), v("g8"), True, True)
+        ts(v("tgl", 0, nc), p0(0, nc), -1.0, Op.mult, 128.0, Op.add)
         act(v("bt", 0, nq), ind(v(bw, 0, 144), v("tgl", 0, nc)))
         mm(v("p4", 0, nq), v("ident"), v("bt", 0, nq), True, True)
         for c, n in chunks:
             mm(part("p5", n, 128 * c, 128 * c + 128, 1), v("bt", 128 * c, 128 * c + n), v("bo14b"), False, False)
-        distances(v("bt", 0, nq), v("p4", 0, nq), "md", "rgn", SU2)
+        distances(v("ctr", 0, nq), "p3", "mc", "rgp", SU1, 256)
+        distances(v("bt", 0, nq), "p4", "md", "rgn", SU2, 0)
         while pend:
             add(pend.pop(0))
         mm(v("p5"), v("ones", 0, 128), v("ckb"), False, True)
@@ -634,7 +640,6 @@ def rank_program(g, core, T, topo):
         cp(v("lm16"), v("lmi"))
         if t == 0:
             constants_d()
-        tt(v("laf"), v("laf"), v("dg"), Op.mult)
         for h in range(2):
             red(v("lac_f", h, h + 1), v("laf", 16 * h, 16 * h + 16), Op.add)
         cp(v("lac"), v("lac_f"))
@@ -670,16 +675,30 @@ def rank_program(g, core, T, topo):
         for k in range(16):
             mm(v("p6", 0, 8), fam("e16f", k), v("pgm", k, 128, 16), k == 0, k == 15)
 
-        ts(v("eq"), v(arr), 0.0, Op.is_ge)
-        tt(v("fa"), v("eq"), v("atab%d" % t), Op.mult)
-        tt(v("wv"), v("fa", 0, 32), v("ownv"), Op.max)
-        tt(v("wb"), v("fa", 32, 64), v("fa", 64, 96), Op.max)
-        tt(v("wv"), v("wv"), v("wb"), Op.max)
-        ts(v("wf"), v("wv"), 8191.5, Op.is_ge)
-        tt(v("rwf"), v("rw"), v("wf"), Op.mult)
-        if not last:
-            tt(v("live", nq, nq + 32), v("go"), v("rwf"), Op.add)
-        ts(v(xb, R0 + 96 * t, R0 + 96 * t + 96), v(arr), 0.0, Op.max)
+        def split_list():
+            tt(v("spa"), v("postp"), v("tr"), Op.subtract)
+            tt(v("spb"), v("spa"), v("go"), Op.mult)
+            tt(v("spa"), v("spb"), v("tr"), Op.add)
+            cp(v("spl16"), v("spa"))
+
+        def split_homes(t=t):
+            tt(v("hw"), v("vst%d" % t, 0, 512, 16), v("p7", 0, 32), Op.add)
+            cp(v("rl16"), v("p6", 0, 8))
+            cp(v("vm", 32 * r, 32 * r + 32), v("hw"))
+            scat(v("hh"), v("spl16"), v("vst%d" % t))
+            scat(v("hh"), v("rl16"), v("vm"))
+
+        def arrival_homes(t=t):
+            ts(v("hd"), v("hw"), -255.0, Op.add)
+            for k in range(3):
+                tt(v("eq", 32 * k, 32 * k + 32), v("fa", 32 * k, 32 * k + 32), v("wv"), Op.is_equal)
+            for k in range(3):
+                tt(v("fa", 32 * k, 32 * k + 32), v("eq", 32 * k, 32 * k + 32), v("hd"), Op.mult)
+            ts(v("hh", R0 + 96 * t, R0 + 96 * t + 96), v("fa"), 255.0, Op.add)
+
+        def homes(t=t):
+            split_homes(t)
+            arrival_homes(t)
 
         def rest(t=t, nq=nq):
             cp(v("wi"), v("wv"))
@@ -695,33 +714,31 @@ def rank_program(g, core, T, topo):
                 act(v("nearf", nq, nq + 32), v("nearp"))
                 scat(v("ctr"), v("pl16"), v("ac"))
                 act(v("ctr", nq, nq + 32), v("bs%d" % t))
-            tt(v("spa"), v("postp"), v("tr"), Op.subtract)
-            tt(v("spb"), v("spa"), v("go"), Op.mult)
-            tt(v("spa"), v("spb"), v("tr"), Op.add)
-            cp(v("spl16"), v("spa"))
-
-        def homes(t=t):
-            tt(v("hw"), v("vst%d" % t, 0, 512, 16), v("p7", 0, 32), Op.add)
-            cp(v("rl16"), v("p6", 0, 8))
-            cp(v("vm", 32 * r, 32 * r + 32), v("hw"))
-            ts(v("hd"), v("hw"), -255.0, Op.add)
-            for k in range(3):
-                tt(v("eq", 32 * k, 32 * k + 32), v("fa", 32 * k, 32 * k + 32), v("wv"), Op.is_equal)
-            for k in range(3):
-                tt(v("fa", 32 * k, 32 * k + 32), v("eq", 32 * k, 32 * k + 32), v("hd"), Op.mult)
-            ts(v("hh", R0 + 96 * t, R0 + 96 * t + 96), v("fa"), 255.0, Op.add)
-            scat(v("hh"), v("spl16"), v("vst%d" % t))
-            scat(v("hh"), v("rl16"), v("vm"))
+                split_list()
 
         if last:
+            split_list()
+            split_homes()
+            dma("y", (T.yh[0:16:2, :], []), (T["hh"][14:128:16, 0:R0], [("hh", 0, R0)]))
+            dma("s", (T.yh[1:16:2, :], []), (T["hh"][15:128:16, 0:R0], [("hh", 0, R0)]))
+
+        ts(v("eq"), v(arr), 0.0, Op.is_ge)
+        tt(v("fa"), v("eq"), v("atab%d" % t), Op.mult)
+        tt(v("wv"), v("fa", 0, 32), v("ownv"), Op.max)
+        tt(v("wb"), v("fa", 32, 64), v("fa", 64, 96), Op.max)
+        tt(v("wv"), v("wv"), v("wb"), Op.max)
+        ts(v("wf"), v("wv"), 8191.5, Op.is_ge)
+        tt(v("rwf"), v("rw"), v("wf"), Op.mult)
+        if not last:
+            tt(v("live", nq, nq + 32), v("go"), v("rwf"), Op.add)
+        ts(v(xb, R0 + 96 * t, R0 + 96 * t + 96), v(arr), 0.0, Op.max)
+        if last:
             rest()
-            homes()
+            arrival_homes()
         else:
             deferred = [rest, homes]
 
     dma("y", (T.ypost[:, :], []), v("postf", 0, 512))
-    dma("y", (T.yh[0:16:2, :], []), (T["hh"][14:128:16, 0:R0], [("hh", 0, R0)]))
-    dma("s", (T.yh[1:16:2, :], []), (T["hh"][15:128:16, 0:R0], [("hh", 0, R0)]))
     ts(v("ya1"), v("x1", R0, R), CF, Op.mult)
     ts(v("ya2"), v("hh", R0, R), N14, Op.mult)
     tt(v("ya3"), v("ya1"), v("ya2"), Op.add)

from concourse.bass import DstId, RemoteDMATransfer
from concourse.mybir import AluOpType as Op, AxisListType as Ax, ActivationFunctionType as Fn

R0, P0, SP, RO = 6144, 416, 32, 3
R = R0 + 96 * RO
PD = 512
MD = 544
WP = 672
XW = 16 * WP
TS = 544
BIG = 262144.0
SU1, SU2 = 15, 12
LEAD, LAG = 5, 4
HQ = (112, 224)
VQ = (64, 128)
AB = [128, 192, 64]

SCRATCH = {}
ALIAS = {}
OWN = ("plr", "pls", "bw", "bs", "mf", "arr", "p0", "p1", "p2", "p3", "p4", "p5", "p6", "p7")


def _b(names, w, dt="bfloat16", where="sbuf"):
    for name in names.split():
        if w > 100 or name.startswith(OWN):
            SCRATCH[name] = (where, [128, w], dt)
        else:
            pool = "small_" + dt
            o = SCRATCH.get(pool, ("", [0, 0]))[1][1]
            ALIAS[name] = (pool, o, w)
            SCRATCH[pool] = ("sbuf", [128, o + (w + 15) // 16 * 16], dt)


F, I, U = "float32", "int32", "uint16"
_b("x1 x2", R)
_b("hh", R + 512)
_b("xd", R0)
_b("xg", XW)
_b("ng mc md", 16 * 480)
_b("e16 rmp rx nm hm vnm", 2048)
_b("e16f", 2048, F)
_b("postI nearI nsh", P0, I)
_b("abI", 1152, I)
_b("ab16", 1152, U)
_b("post16 near16", 512, U)
_b("postf nearf", WP, F)
_b("slot", P0, F)
_b("ctr live", WP)
for _t in range(RO):
    _b("tab%d" % _t, 4 * TS)
    _b("plr%d" % _t, 6, U)
    _b("pls%d" % _t, 2, U)
    _b("bw%d" % _t, 144)
    _b("bs%d" % _t, 32)
    _b("mf%d" % _t, 128)
    _b("arr%d" % _t, 96)
    _b("atab%d" % _t, 96, F)
    _b("vst%d" % _t, 512)
_b("full scan sd1 junk", TS)
_b("cmpv", TS + 2)
_b("cidx", TS, F)
_b("ident nid ibig bo bo14c bo14b bo14p bo14n px mw mw15 one0 lga u128 w128 w128b vm oh lgt lut dat", 128)
_b("bof zx pg pgm", 128, F)
_b("lg", 1024)
_b("ones n15 ck cka ckb wt tq ff xs xs2 ma mb vhi vlo", 512)
_b("bt", 480)
_b("kt k1", 256, F)
_b("k2", 128, F)
_b("k3", 64, F)
_b("fc", 64, F)
_b("km kmf i32k dg tr whi postp nearp laf lbf ktk spa spb ownv ra wv wb wd hd fo", 32, F)
_b("kmi kma wi wr", 32, I)
_b("k16 lp oa obt ob go nog rw rwf wf ac lpn hw z32", 32)
_b("g8 rgp rgn", 8)
_b("miw", 16)
_b("pcol pr", 2, I)
_b("i16 r16", 16, F)
_b("i8 cs ms", 8, F)
_b("acc lac_f lbc_f kmx", 2, F)
_b("pl16 lac lbc", 2, U)
_b("la16 ps16 lb16 spl16 tgl", 32, U)
_b("ls16 lq16 lm16 rl16", 8, U)
_b("lsi lqi lmi", 8, I)
_b("fa eq", 96, F)
_b("ya1 ya2 ya3", 288)
for _i in range(8):
    _b("p%d" % _i, 512, F, "psum")

NDMA = 16
SEMAPHORES = ["qv", "qs", "qp", "qg", "sent"] + ["d%d" % i for i in range(NDMA)] + \
    ["%s%d" % (a, t) for a in ("rp", "rb", "rm") for t in range(RO)]


def rank_program(g, core, T, topo):
    r = T.rank_of(core)
    if r is None:
        return
    Q = {"v": g.vector, "s": g.scalar, "p": g.tensor, "g": g, "y": g.sync}
    cnt = {"qv": 0, "qs": 0, "qp": 0, "qg": 0}
    total = {}
    known = {q: {} for q in Q}
    acc = {}
    dn = [0]

    def waits(q, toks):
        need = {}
        for (sem, val, q2, snap) in toks:
            if known[q].get(sem, 0) < val and (sem not in need or need[sem][1] < val):
                need[sem] = (sem, val, q2, snap)
        lst = list(need.values())
        for tk in lst:
            if any(o is not tk and o[3].get(tk[0], 0) >= tk[1] for o in lst):
                continue
            Q[q].wait_ge(T.sem[tk[0]], tk[1])
        for tk in lst:
            k = known[q]
            k[tk[0]] = max(k.get(tk[0], 0), tk[1])
            for s2, v2 in tk[3].items():
                if k.get(s2, 0) < v2:
                    k[s2] = v2

    def deps(q, reads, writes):
        toks = []
        for is_w, regs in ((False, reads), (True, writes)):
            for (b, c0, c1) in regs:
                ps = SCRATCH.get(b, ("",))[0] == "psum"
                for (d0, d1, w2, tok) in acc.get(b, ()):
                    if ps:
                        if tok[2] == q and (q == "p" or not (is_w or w2)):
                            continue
                        toks.append(tok)
                    elif d0 < c1 and c0 < d1 and (is_w or w2):
                        toks.append(tok)
        return toks

    def note(reads, writes, tok):
        for (b, c0, c1) in writes:
            ps = SCRATCH.get(b, ("",))[0] == "psum"
            old = acc.get(b, [])
            acc[b] = [o for o in old if not (ps or (c0 <= o[0] and o[1] <= c1))] + [(c0, c1, True, tok)]
        for (b, c0, c1) in reads:
            old = acc.get(b, [])
            acc[b] = [o for o in old if not (not o[2] and o[3][2] == tok[2] and o[3][0] == tok[0] and c0 <= o[0] and o[1] <= c1)] + [(c0, c1, False, tok)]

    def run(q, fn, reads, writes):
        waits(q, deps(q, reads, writes))
        sem = "q" + q
        cnt[sem] += 1
        total[sem] = cnt[sem]
        fn().then_inc(T.sem[sem], 1)
        note(reads, writes, (sem, cnt[sem], q, dict(known[q])))

    def dma(q, out, in_):
        waits(q, deps(q, in_[1], out[1]))
        sem = "d%d" % dn[0]
        dn[0] += 1
        Q[q].dma_start(out[0], in_[0]).then_inc(T.sem[sem], 16)
        total[sem] = 16
        note(in_[1], out[1], (sem, 16, "dma", dict(known[q])))

    def v(b, c0=0, c1=None, s=1):
        if b in ALIAS:
            b, o, w = ALIAS[b]
            c0, c1 = o + c0, o + (w if c1 is None else c1)
        c1 = SCRATCH[b][1][1] if c1 is None else c1
        return (T[b][:, c0:c1] if s == 1 else T[b][:, c0:c1:s], [(b, c0, c1)])

    def part(b, n, c0, c1, s):
        return (T[b][0:n, c0:c1] if s == 1 else T[b][0:n, c0:c1:s], [(b, c0, c1)])

    def ind(win, off):
        return (win[0].indirect(off[0]), win[1] + off[1])

    def col(i):
        return v("fc", i, i + 1)

    def fam(b, m):
        return v(b, 128 * m, 128 * m + 128)

    def tt(out, a, b, op):
        run("v", lambda: g.vector.tensor_tensor(out[0], a[0], b[0], op), a[1] + b[1], out[1])

    def ts(out, a, s1, o1, s2=None, o2=None):
        regs = list(a[1])
        x1, x2 = s1, s2
        if isinstance(s1, tuple):
            regs += s1[1]
            x1 = s1[0]
        if isinstance(s2, tuple):
            regs += s2[1]
            x2 = s2[0]
        if o2 is None:
            run("v", lambda: g.vector.tensor_scalar(out[0], a[0], x1, None, o1), regs, out[1])
        else:
            run("v", lambda: g.vector.tensor_scalar(out[0], a[0], x1, x2, o1, o2), regs, out[1])

    def cp(out, a):
        run("v", lambda: g.vector.tensor_copy(out[0], a[0]), a[1], out[1])

    def scat(win, off, a):
        run("v", lambda: g.vector.tensor_copy(win[0].indirect(off[0]), a[0]), a[1] + off[1] + win[1], win[1])

    def red(out, a, op, ab=False):
        kw = {"apply_absolute_value": True} if ab else {}
        run("v", lambda: g.vector.tensor_reduce(out[0], a[0], Ax.X, op, **kw), a[1], out[1])

    def tr(out, a):
        run("v", lambda: g.vector.transpose(out[0], a[0]), a[1], out[1])

    def fill(out, c):
        run("v", lambda: g.vector.memset(out[0], c), [], out[1])

    def act(out, a, fn=Fn.Copy, bias=None, scale=None, accum=None):
        kw = {}
        regs = list(a[1])
        w = list(out[1])
        if bias is not None:
            kw["bias"] = bias[0]
            regs += bias[1]
        if isinstance(scale, tuple):
            kw["scale"] = scale[0]
            regs += scale[1]
        elif scale is not None:
            kw["scale"] = scale
        if accum is not None:
            kw["accum_out"] = accum[0]
            w += accum[1]
        run("s", lambda: g.scalar.activation(out[0], a[0], fn, **kw), regs, w)

    def mm(out, lhsT, rhs, start, stop):
        run("p", lambda: g.tensor.matmul(out[0], lhsT[0], rhs[0], start, stop), lhsT[1] + rhs[1], out[1])

    def iota(out, pat, base=0, cm=0, flag=True):
        kw = {"allow_small_or_imprecise_dtypes": True} if flag else {}
        run("g", lambda: g.iota(out[0], pat, base, cm, **kw), [], out[1])

    others = [q for q in range(len(T.cores)) if q != r]
    NE = 2

    def send(bufs, dsts, sem):
        trs = []
        regs = []
        for i, q in enumerate(others):
            dst = T.cores[q]
            rid, pid, _ = topo.addr(dst)
            eng = topo.engines(core, dst)[NE * i:NE * i + NE]
            trs.append(RemoteDMATransfer(dst_ids=[DstId(rid=rid, pnc=pid)], dma_engine_mask=sum(1 << e for e in eng),
                                         remote_sem=T.sem[sem], srcs=[bufs[i][0]], dsts=[dsts[i][0]]))
            regs += bufs[i][1]
        waits("g", deps("g", regs, []))
        g.remote_dma_fused(trs, local_sem=T.sem["sent"])
        total["sent"] = total.get("sent", 0) + NE * len(others)

    def arrives(regs, sem):
        n = NE * len(others)
        total[sem] = n
        note([], regs, (sem, n, "remote", {}))

    def place(q):
        return r - (1 if r > q else 0)

    half = R0 // 2
    dma("y", v("postI"), (T.post[:, :], []))
    dma("s", v("hh", 0, half), (T.rec[:, 0:half], []))
    dma("y", v("hh", half, R0), (T.rec[:, half:R0], []))
    dma("s", v("abI"), (T.absorb[:, :], []))
    dma("y", v("nearI"), (T.near[:, :], []))
    dma("s", v("xd", 0, half), (T.rec[:, 0:half], []))
    dma("y", v("xd", half, R0), (T.rec[:, half:R0], []))
    dma("y", v("ctr", 0, P0), (T.cen[:, :], []))

    pI, p15 = v("pcol", 0, 1), v("pcol", 1, 2)
    NI = v("vnm", 0, 128)
    R1 = v("md", 0, 2048)
    iota(pI, [[0, 1]], 0, 1, False)
    iota(v("vnm"), [[-1, 16], [1, 128]])
    iota(v("i32k"), [[16, 32]])
    iota(v("w128"), [[-1, 128]], 128)
    iota(v("slot"), [[16, P0]])
    iota(v("whi"), [[8, 4], [0, 8]])
    iota(v("n15"), [[0, 32], [1, 16]])
    iota(v("i16"), [[1, 16]])
    iota(v("i8"), [[16, 8]])
    iota(v("cidx"), [[1, TS]])
    iota(v("dg"), [[0, 2], [1, 16]])
    iota(v("postf", MD, WP), [[1, 128]], R)
    iota(v("postf", PD, MD), [[0, 32]])
    iota(v("tab0"), [[0, 4 * TS]])
    fill(v("hh", R0, R), 0.0)
    fill(v("live", P0, WP), 0.0)
    fill(v("full", P0, TS), 0.0)
    fill(v("cmpv", TS, TS + 2), -544.0)
    fill(v("ctr", P0, WP), 0.0)
    fill(v("nearf", P0, WP), 0.0)
    fill(v("wt"), 0.0)
    fill(v("ff", P0, 512), 0.0)
    fill(v("ones"), 1.0)
    fill(v("z32"), 0.0)
    PF, MF_, PB = col(0), col(1), col(2)
    ts(p15, pI, 15, Op.bitwise_and)
    cp(PF, pI)
    cp(MF_, p15)
    tt(PB, PF, MF_, Op.subtract)
    for i in range(7):
        ts(col(8 + i), MF_, float(i), Op.is_equal)
    C14, C15, N14, CF = col(16), col(17), col(18), col(19)
    ts(C14, MF_, 14.0, Op.is_equal)
    ts(C15, MF_, 15.0, Op.is_equal)
    ts(CF, MF_, 13.5, Op.is_le)
    ts(N14, MF_, 13.5, Op.is_gt)
    ts(col(20), C14, 256.0, Op.mult, C15, Op.add)
    K32, KN32, KN16, K16c = col(21), col(22), col(23), col(24)
    ts(K32, CF, 32.0, Op.mult)
    ts(KN32, CF, -32.0, Op.mult)
    ts(KN16, CF, -16.0, Op.mult)
    ts(K16c, CF, 16.0, Op.mult)
    HB, HB1 = col(26), col(27)
    ts(HB, MF_, 0.5, Op.add)
    ts(HB1, MF_, 16.5, Op.add)
    ts(v("e16"), v("vnm"), PB, Op.is_equal)
    act(v("hm"), v("e16"), scale=col(20))
    cp(v("post16", 0, P0), v("postI"))

    X = v("hh", 0, R)
    ts(col(37), PF, 0.0, Op.mult, -256.0, Op.add)
    act(v("slot"), v("slot"), Fn.Identity, bias=MF_)
    act(R1, v("e16"), Fn.Identity, scale=0.0, bias=col(37))
    home_parts = ((0, HQ[0], "p5"), (HQ[0], HQ[1], "p2"), (HQ[1], P0, "p6"))
    for (a, b, pb) in home_parts[0:2]:
        act(v("xg", 16 * a, 16 * b), ind(X, v("post16", a, b)))
    ts(v("u128"), NI, PB, Op.subtract)
    ts(v("px"), v("u128"), 0.0, Op.is_ge)
    ts(v("w128b"), v("u128"), 15.5, Op.is_le)
    tt(v("bo"), v("px"), v("w128b"), Op.mult)
    cp(v("postf", 0, P0), v("postI"))
    ts(v("g8"), v("i8"), PB, Op.is_equal)
    act(v("rgp"), v("g8"), scale=K32)
    act(v("rgn"), v("g8"), scale=KN32)
    act(v("bo14p"), v("bo"), scale=K16c)
    act(v("bo14n"), v("bo"), scale=KN16)
    A, B = col(33), col(34)
    ts(A, col(12), 32768.0, Op.mult)
    ts(A, col(14), 16.0, Op.mult, A, Op.add)
    ts(B, col(8), 32768.0, Op.mult, col(9), Op.add)
    for (i, w) in ((10, -256.0), (11, -16.0), (12, -32768.0 * 128), (13, -15.0)):
        ts(B, col(i), w, Op.mult, B, Op.add)
    ts(v("lga"), NI, A, Op.mult, B, Op.add)
    for k in range(8):
        ts(col(40 + k), PB, 16.0 * k, Op.is_equal)
    for k in range(8):
        act(v("lg", 128 * k, 128 * k + 128), v("lga"), scale=col(40 + k))
    cp(v("xg", 16 * HQ[1], 16 * P0), ind(X, v("post16", HQ[1], P0)))
    for (a, b, pb) in (home_parts[0], home_parts[2], home_parts[1]):
        for m in range(16):
            mm(v(pb, a, b), fam("hm", m), v("xg", 16 * a + m, 16 * b, 16), m == 0, m == 15)
    ts(col(28), MF_, 512.0, Op.add)
    ts(col(29), MF_, 528.0, Op.add)
    ts(v("scan"), v("cidx"), col(28), Op.is_ge, 16.0, Op.mult)
    ts(v("sd1"), v("cidx"), col(29), Op.is_ge, 84.0, Op.mult)
    tt(v("sd1"), v("sd1"), v("scan"), Op.add)
    ts(v("ident"), NI, PF, Op.is_equal)
    ts(v("ibig"), v("ident"), BIG, Op.mult)
    ts(v("nid"), v("ident"), -1.0, Op.mult)
    ts(v("w128b"), NI, PF, Op.is_gt, -32.0, Op.mult)
    tt(v("w128b"), v("w128b"), v("bo"), Op.mult)
    tt(v("px"), v("w128b"), v("ident"), Op.add)
    ts(v("mw"), v("bo"), MF_, Op.mult)
    ts(col(30), PF, 0.0, Op.is_equal)
    ts(col(31), PF, 1.0, Op.is_equal)
    ts(col(32), col(30), -BIG, Op.mult)
    ts(v("one0"), NI, 0.0, Op.mult, col(30), Op.add)
    cp(v("k16"), v("i32k"))
    ts(v("dat"), v("w128"), col(8), Op.mult, col(9), Op.add)
    ts(v("ckb"), v("n15"), -1.0, Op.mult, 15.0, Op.add)
    ts(v("ckb"), v("ckb"), col(31), Op.mult)
    ts(v("cka"), v("n15"), 0.0, Op.mult, col(32), Op.add)
    ts(v("ck"), v("ckb"), col(32), Op.add)
    ts(v("dg"), v("dg"), MF_, Op.is_equal)
    for (a, b, pb) in (home_parts[0], home_parts[2], home_parts[1]):
        tt(v("live", a, b), v("slot", a, b), v(pb, a, b), Op.is_equal)

    def constants_b():
        ts(v("nsh"), v("nearI"), 4, Op.arith_shift_right, 96, Op.bitwise_and)
        tt(v("nearf", 0, P0), v("nsh"), v("nearI"), Op.add)
        cp(v("near16", 0, P0), v("nearf", 0, P0))
        cp(v("ab16"), v("abI"))
        act(v("rx"), v("e16"), scale=KN16)
        act(v("rmp"), v("e16"), scale=K32)
        act(v("nm"), v("e16"), scale=col(8))
        run("g", lambda: g.affine_select(R1[0], R1[0], [[-1, 16], [1, 128]], Op.is_gt, 0.0, 1, -1), R1[1], R1[1])
        run("g", lambda: g.affine_select(R1[0], R1[0], [[0, 16], [-1, 128]], Op.is_gt, 0.0, 15, 1), R1[1], R1[1])
        dma("y", (T["nm"][1:128:16, :], [("nm", 0, 2048)]), (T["md"][1:128:16, 0:2048], R1[1]))

    def constants_c():
        ts(v("u128"), v("n15", 0, 128), SU1 - 0.5, Op.is_ge, -2.0, Op.mult)
        ts(v("u128"), v("u128"), 1.0, Op.add)
        tt(v("bo14c"), v("u128"), v("bo14n"), Op.mult)
        ts(v("u128"), v("n15", 0, 128), SU2 - 0.5, Op.is_ge, -2.0, Op.mult)
        ts(v("u128"), v("u128"), 1.0, Op.add)
        tt(v("bo14b"), v("u128"), v("bo14p"), Op.mult)
        ts(v("pr", 0, 1), pI, 4, Op.arith_shift_right)
        cp(col(35), v("pr", 0, 1))
        ts(v("wt", 2, 512, 16), v("whi"), col(35), Op.add)
        ts(v("wt", 3, 512, 16), v("whi"), 0.0, Op.mult, MF_, Op.add)
        for k in (4, 5):
            ts(v("wt", k, 512, 16), v("whi"), 0.0, Op.mult, 1.0, Op.add)
        ts(col(36), col(10), -34.0, Op.mult, col(14), Op.add)
        cp(v("tq", 31, 32), col(36))
        ts(v("r16"), v("i16"), MF_, Op.is_equal)
        ts(v("cs"), v("i8"), PB, Op.is_equal)
        ts(v("miw"), v("i16"), MF_, Op.is_equal)

    def constants_d():
        act(v("e16f"), v("e16"))
        iota(v("vhi"), [[1, 2], [0, 256]], 26)
        iota(v("vlo"), [[0, 2], [1, 256]])
        for k in range(RO):
            iota(v("atab%d" % k), [[32 - 8192, 3], [1, 32]], 3 * 8192 + R0 + 96 * k)
        for k in range(1, RO):
            iota(v("tab%d" % k), [[0, 4 * TS]])
        ts(v("w128b"), v("n15", 0, 128), 15.0, Op.is_equal)
        tt(v("mw15"), v("mw"), v("w128b"), Op.mult)
        cp(v("bof"), v("bo"))
        ts(v("tr"), v("i32k"), MF_, Op.add, float(R), Op.add)
        fill(v("vm"), 255.0)
        ts(v("vst0"), v("vhi"), C14, Op.mult)
        ts(v("vlo"), v("vlo"), C15, Op.mult)
        tt(v("vst0"), v("vst0"), v("vlo"), Op.add)
        for t in range(1, RO):
            ts(col(36 + t), C14, 2.0 * t, Op.mult)
            act(v("vst%d" % t), v("vst0"), Fn.Identity, bias=col(36 + t))

    deferred = []

    for t in range(RO):
        nq = P0 + SP * t
        nc = nq // 16
        last = t == RO - 1
        xa = ["hh", "x1", "x2"][t]
        xb = ["x1", "x2", "x1"][t]
        Xa = v(xa, 0, R)
        Xb = v(xb, 0, R)
        tab, plr, pls, bw, bs, mf, arr = [n + str(t) for n in ("tab", "plr", "pls", "bw", "bs", "mf", "arr")]
        p0 = lambda a=0, b=512: v("p0", a, b)
        p1 = lambda a=0, b=512: v("p1", a, b)

        mm(p0(0, nq), v("bo"), v("live", 0, nq), True, True)
        ts(v("full", 0, nq), p0(0, nq), 13.5, Op.is_ge)
        run("v", lambda: g.vector.tensor_tensor_scan(v("scan")[0], v("full")[0], v("sd1")[0], 0.0, Op.add, Op.max),
            v("full")[1] + v("sd1")[1], v("scan")[1])
        act(v("junk"), v("scan"), Fn.Sign, bias=HB, scale=-1.0, accum=v("acc", 0, 1))
        ts(v("cmpv", 0, TS), v("scan"), HB1, Op.is_le, 2.0, Op.mult)
        red(v("acc", 1, 2), v("cmpv", 0, TS + 1), Op.add)
        ts(v(pls), v("acc"), 0.5, Op.mult, 272.0 + TS * r, Op.add)
        send([v(pls)] * 3, [v("plr%d" % t, 2 * place(q), 2 * place(q) + 2) for q in others], "rp%d" % t)
        arrives([(plr, 0, 6)], "rp%d" % t)
        if t > 0:
            deferred[0]()
        ts(v("pl16"), v("acc"), 0.5, Op.mult, 272.0, Op.add)
        scat(v(tab), v(pls), v("dat", 32 * r, 32 * r + 32))
        cp(v("lp"), ind(v("live"), v("pl16")))
        cp(v("postp"), ind(v("postf"), v("pl16")))
        cp(v("ps16"), v("postp"))
        mm(p1(0, 32), v("px"), v("lp"), True, True)
        scat(v("live"), v("pl16"), v("z32"))
        if t == 0:
            constants_b()
        pieces = []
        a = 384 * t
        o = 0
        for w in AB:
            pieces.append((a, a + w, 16 * o))
            a += w
            o += w

        def absorb(i):
            a, b, c = pieces[i]
            w = 16 * (b - a)
            tt(v(xb, c, c + w), ind(Xa, v("ab16", a, b)), v("xd", c, c + w), Op.max)

        absorb(0)
        act(v(xb, R0, R), v(xa, R0, R))
        ts(v("oa"), p1(0, 32), 0.0, Op.max)
        mm(p0(0, 32), v("mw"), v("oa"), True, False)
        mm(p0(0, 32), v("one0"), v("k16"), False, True)
        cp(v("la16"), p0(0, 32))
        tt(v("laf"), v("dg"), p0(0, 32), Op.mult)
        for (c0, c1, d0, d1) in ((0, 2 * r, 0, 32 * r), (2 * r, 6, 32 * r + 32, 128)):
            if c1 > c0:
                scat(v(tab), v(plr, c0, c1), v("dat", d0, d1))
        qh = (nq // 2) // 16 * 16
        halves = ((0, qh, "p2"), (qh, nq, "p6"))
        for (qa, qb, pn) in halves:
            act(v("ng", 16 * qa, 16 * qb), ind(v(tab), v("near16", qa, qb)))
        for i in range(1, len(pieces)):
            absorb(i)
        XS = v("xs")
        cp(XS, ind(Xb, v("ps16")))
        cp(v("xs2"), XS)
        tt(v("ma"), ind(XS, v("la16")), v("xs2"), Op.max)
        cp(v("xg", 0, 16 * VQ[0]), ind(Xb, v("post16", 0, VQ[0])))
        mm(p1(0, 32), v("ck", 0, 128), v("ones", 0, 32), True, False)
        mm(p1(0, 32), v("ibig"), v("lp"), False, False)
        for m in range(16):
            mm(p1(0, 32), fam("rx", m), v("xs", m, 512, 16), False, False)
        for m in range(16):
            mm(p1(0, 32), fam("rmp", m), v("ma", m, 512, 16), False, m == 15)
        tr(v("ktk"), p1(0, 32))
        for h in range(2):
            red(v("kmx", h, h + 1), v("ktk", 16 * h, 16 * h + 16), Op.max)
        for h in range(2):
            ts(v("obt", 16 * h, 16 * h + 16), v("ktk", 16 * h, 16 * h + 16), v("kmx", h, h + 1), Op.is_equal)
        tr(v("ob"), v("obt"))
        mm(p0(0, 32), v("mw"), v("ob"), True, False)
        mm(p0(0, 32), v("one0"), v("k16"), False, True)
        tt(v("lbf"), v("dg"), p0(0, 32), Op.mult)
        for h in range(2):
            red(v("lbc_f", h, h + 1), v("lbf", 16 * h, 16 * h + 16), Op.add)
        cp(v("lbc"), v("lbc_f"))
        cp(v(bs), ind(XS, v("lbc")))
        send([v(bs)] * 3, [v("bw%d" % t, 32 * r, 32 * r + 32)] * 3, "rb%d" % t)
        if not last:
            dma("y", v("xd"), v(xb, 0, R0))
        cp(v("lb16"), p0(0, 32))
        cp(v(bw, 32 * r, 32 * r + 32), v(bs))
        fill(v(bw, 128, 144), 8192.0)
        for q in others:
            arrives([(bw, 32 * q, 32 * q + 32)], "rb%d" % t)

        if t == 0:
            act(v("hm"), v("e16"), scale=KN32)
            iota(v("xg", 16 * P0, XW), [[0, XW - 16 * P0]], -1)
        for (a, b) in ((VQ[1], 256), (256, nq)):
            act(v("xg", 16 * a, 16 * b), ind(Xb, v("post16", a, b)))
        if t > 0:
            deferred[1]()
        for (qa, qb, pn) in halves:
            for j in range(16):
                mm(v(pn, qa, qb), fam("nm", j), v("ng", 16 * qa + j, 16 * qb, 16), j == 0, j == 15)
            act(v("ff", qa, qb), v(pn, qa, qb), Fn.Relu)
        cp(v("xg", 16 * VQ[0], 16 * VQ[1]), ind(Xb, v("post16", VQ[0], VQ[1])))
        if t == 0:
            constants_c()
        mm(v("p3", 0, nq), v("ident"), v("ctr", 0, nq), True, True)

        chunks = [(c, min(nq, 128 * c + 128) - 128 * c) for c in range(4)]
        mm(v("p5"), v("ones", 0, 128), v("cka"), True, False)
        for c in range(4):
            gc = v("p5", 128 * c, 128 * c + 128)
            mm(gc, v("live", 128 * c, 128 * c + 128), v("ibig"), False, False)
            mm(gc, v("ctr", 128 * c, 128 * c + 128), v("bo14c"), False, False)
        flip = [0]
        pend = []

        def xm(m, a=0, b=nq):
            return v("xg", 16 * a + m, 16 * b, 16)

        def s_unit(m, other, dst, sums):
            pb = ("p6", "p7", "p1")[flip[0] % 3]
            flip[0] += 1
            mm(v(pb, 0, nq), v("ident"), xm(m), True, False)
            mm(v(pb, 0, nq), v("nid"), other, False, True)
            act(v(dst, m * 480, m * 480 + nq), v(pb, 0, nq), Fn.Relu)
            return (sums, m, dst, chunks)

        def add(u):
            sums, m, dst, cs = u
            for c, n in cs:
                mm(part("p5", n, 128 * c + m, 128 * c + 128, 16), v(dst, m * 480 + 128 * c, m * 480 + 128 * c + n), v(sums), False, False)

        def pipe(u):
            pend.append(u)
            if len(pend) > LAG:
                add(pend.pop(0))

        def v_unit(m, pb, dst, sums, a, b):
            tt(v(dst, m * 480 + a, m * 480 + b), xm(m, a, b), v(pb, a, b), Op.max)
            pipe((sums, m, dst, [x for x in chunks if a <= 128 * x[0] < b]))

        def distances(other, pb, dst, sums, su, a):
            vm_ = list(range(su))
            sm_ = list(range(su, 16))
            while vm_ or sm_:
                if sm_ and (not vm_ or len(sm_) * su >= (len(vm_) - LEAD) * (16 - su)):
                    pipe(s_unit(sm_.pop(0), other, dst, sums))
                else:
                    v_unit(vm_.pop(0), pb, dst, sums, a, nq)

        for m in range(SU1):
            v_unit(m, "p3", "mc", "rgp", 0, 256)
        for k in range(16):
            mm(p0(0, nc), fam("e16", k), v("ff", k, nq, 16), k == 0, k == 15)
        for c in range(4):
            mm(v("p2", 8 * c, 8 * c + 8), v("ff", 128 * c, 128 * c + 128), v("g8"), True, True)
        ts(v("tgl", 0, nc), p0(0, nc), -1.0, Op.mult, 128.0, Op.add)
        act(v("bt", 0, nq), ind(v(bw, 0, 144), v("tgl", 0, nc)))
        mm(v("p4", 0, nq), v("ident"), v("bt", 0, nq), True, True)
        for c, n in chunks:
            mm(part("p5", n, 128 * c, 128 * c + 128, 1), v("bt", 128 * c, 128 * c + n), v("bo14b"), False, False)
        distances(v("ctr", 0, nq), "p3", "mc", "rgp", SU1, 256)
        distances(v("bt", 0, nq), "p4", "md", "rgn", SU2, 0)
        while pend:
            add(pend.pop(0))
        mm(v("p5"), v("ones", 0, 128), v("ckb"), False, True)

        cp(v("kt"), v("p5", 1, 512, 2))
        tt(v("k1"), v("p5", 0, 512, 2), v("kt"), Op.max)
        prev, w = "k1", 256
        for nxt in ("k2", "k3", "km"):
            w //= 2
            tt(v(nxt), v(prev, 0, 2 * w, 2), v(prev, 1, 2 * w, 2), Op.max)
            prev = nxt
        cp(v("kmi"), v("km"))
        ts(v("kmf"), v("km"), 15.5, Op.is_ge)
        ts(v("kma"), v("kmi"), 15, Op.bitwise_and)
        tt(v("wt", 0, 512, 16), v("kmf"), v("p2", 0, 32), Op.mult)
        cp(v("wt", 1, 512, 16), v("kma"))
        for c in range(4):
            mm(v("p%d" % (c // 2), 128 * (c % 2), 128 * (c % 2) + 128), v("wt", 128 * c, 128 * c + 128), v("ident"), True, True)
        cp(v("tq", 32, 288), v("p0", 0, 256))
        act(v("tq", 288, 32 + nq), v("p1", 0, nq - 256))
        banks = ["p3", "p4", "p2", "p6", "p7", "p0", "p1", "p5"]
        for k in range(8):
            mm(v(banks[k], 0, nq + 1), v("lg", 128 * k, 128 * k + 128), v("tq", 31, 32 + nq), True, True)
        for k in range(8):
            red(v("ms", k, k + 1), v(banks[k], 0, nq + 1), Op.min, True)
            act(v("zx", 16 * k, 16 * k + 16), v("r16"), scale=v("ms", k, k + 1))
        mm(p0(0, 8), v("zx"), v("cs"), True, True)
        cp(v("ls16"), p0(0, 8))
        cp(v(mf), ind(v("xg"), v("ls16")))
        send([v(mf, 32 * q, 32 * q + 32) for q in others],
             [v("arr%d" % t, 32 * place(q), 32 * place(q) + 32) for q in others], "rm%d" % t)
        arrives([(arr, 0, 96)], "rm%d" % t)

        tt(v("mb"), ind(XS, v("lb16")), v("xs2"), Op.max)
        cp(v("lsi"), p0(0, 8))
        ts(v("lqi"), v("lsi"), 4, Op.arith_shift_right)
        ts(v("lmi"), v("lsi"), 15, Op.bitwise_and)
        cp(v("lq16"), v("lqi"))
        cp(v("lm16"), v("lmi"))
        if t == 0:
            constants_d()
        for h in range(2):
            red(v("lac_f", h, h + 1), v("laf", 16 * h, 16 * h + 16), Op.add)
        cp(v("lac"), v("lac_f"))
        act(v("ac"), ind(XS, v("lac")))
        if not last:
            act(v("lgt"), ind(v("live"), v("lq16")))
        act(v("oh"), ind(v("miw"), v("lm16")))
        act(v("pg"), ind(v("postf"), v("lq16")))
        mm(p1(0, 32), v("ck", 0, 128), v("ones", 0, 32), True, False)
        mm(p1(0, 32), v("ibig"), v("lp"), False, False)
        for m in range(16):
            mm(p1(0, 32), fam("rmp", m), v("ma", m, 512, 16), False, False)
        for m in range(16):
            mm(p1(0, 32), fam("hm", m), v("mb", m, 512, 16), False, False)
        mm(p1(0, 32), v("bo14p"), v(bs), False, False)
        mm(p1(0, 32), v("bo14n"), v("ac"), False, True)
        if not last:
            tt(v("lut"), v("lgt"), v("oh"), Op.subtract)
            scat(v("live"), v("lq16"), v("lut"))
        ts(v("go"), p1(0, 32), 15.5, Op.is_ge)
        ts(v("nog"), p1(0, 32), 15.5, Op.is_lt)
        mm(p0(0, 32), v("px"), v("nog"), True, True)
        tt(v("pgm"), v("pg"), v("oh"), Op.mult)
        mm(v("p4", 0, 32), v("bof"), v("pgm", 32 * r, 32 * r + 32), True, True)
        if not last:
            tt(v("lpn"), v("lp"), v("go"), Op.subtract)
            scat(v("live"), v("pl16"), v("lpn"))
        ts(v("rw"), p0(0, 32), 0.0, Op.max)
        ts(v("fo"), v(mf, 32 * r, 32 * r + 32), 0.0, Op.is_ge, 2.0 ** -17, Op.max)
        ts(v("ra"), v("p4", 0, 32), 32768.0, Op.add)
        tt(v("ownv"), v("ra"), v("fo"), Op.mult)
        mm(v("p7", 0, 32), v("mw15"), v("rw"), True, True)
        for k in range(16):
            mm(v("p6", 0, 8), fam("e16f", k), v("pgm", k, 128, 16), k == 0, k == 15)

        def split_list():
            tt(v("spa"), v("postp"), v("tr"), Op.subtract)
            tt(v("spb"), v("spa"), v("go"), Op.mult)
            tt(v("spa"), v("spb"), v("tr"), Op.add)
            cp(v("spl16"), v("spa"))

        def split_homes(t=t):
            tt(v("hw"), v("vst%d" % t, 0, 512, 16), v("p7", 0, 32), Op.add)
            cp(v("rl16"), v("p6", 0, 8))
            cp(v("vm", 32 * r, 32 * r + 32), v("hw"))
            scat(v("hh"), v("spl16"), v("vst%d" % t))
            scat(v("hh"), v("rl16"), v("vm"))

        def arrival_homes(t=t):
            ts(v("hd"), v("hw"), -255.0, Op.add)
            for k in range(3):
                tt(v("eq", 32 * k, 32 * k + 32), v("fa", 32 * k, 32 * k + 32), v("wv"), Op.is_equal)
            for k in range(3):
                tt(v("fa", 32 * k, 32 * k + 32), v("eq", 32 * k, 32 * k + 32), v("hd"), Op.mult)
            ts(v("hh", R0 + 96 * t, R0 + 96 * t + 96), v("fa"), 255.0, Op.add)

        def homes(t=t):
            split_homes(t)
            arrival_homes(t)

        def rest(t=t, nq=nq):
            cp(v("wi"), v("wv"))
            ts(v("wr"), v("wi"), 8191, Op.bitwise_and)
            cp(v("wd"), v("wr"))
            tt(v("wb"), v("wd"), v("postp"), Op.subtract)
            tt(v("wd"), v("wb"), v("rwf"), Op.mult)
            tt(v("postf", nq, nq + 32), v("wd"), v("postp"), Op.add)
            if t < RO - 1:
                cp(v("post16", nq, nq + 32), v("postf", nq, nq + 32))
                act(v("nearp"), ind(v("nearf"), v("pl16")))
                cp(v("near16", nq, nq + 32), v("nearp"))
                act(v("nearf", nq, nq + 32), v("nearp"))
                scat(v("ctr"), v("pl16"), v("ac"))
                act(v("ctr", nq, nq + 32), v("bs%d" % t))
                split_list()

        if last:
            split_list()
            split_homes()
            dma("y", (T.yh[0:16:2, :], []), (T["hh"][14:128:16, 0:R0], [("hh", 0, R0)]))
            dma("s", (T.yh[1:16:2, :], []), (T["hh"][15:128:16, 0:R0], [("hh", 0, R0)]))

        ts(v("eq"), v(arr), 0.0, Op.is_ge)
        tt(v("fa"), v("eq"), v("atab%d" % t), Op.mult)
        tt(v("wv"), v("fa", 0, 32), v("ownv"), Op.max)
        tt(v("wb"), v("fa", 32, 64), v("fa", 64, 96), Op.max)
        tt(v("wv"), v("wv"), v("wb"), Op.max)
        ts(v("wf"), v("wv"), 8191.5, Op.is_ge)
        tt(v("rwf"), v("rw"), v("wf"), Op.mult)
        if not last:
            tt(v("live", nq, nq + 32), v("go"), v("rwf"), Op.add)
        ts(v(xb, R0 + 96 * t, R0 + 96 * t + 96), v(arr), 0.0, Op.max)
        if last:
            rest()
            arrival_homes()
        else:
            deferred = [rest, homes]

    dma("y", (T.ypost[:, :], []), v("postf", 0, 512))
    ts(v("ya1"), v("x1", R0, R), CF, Op.mult)
    ts(v("ya2"), v("hh", R0, R), N14, Op.mult)
    tt(v("ya3"), v("ya1"), v("ya2"), Op.add)
    dma("y", (T.ya[:, :], []), v("ya3"))
    for sem, val in total.items():
        g.wait_ge(T.sem[sem], val)
